import numpy as np
import ml_dtypes


def mxq(x, axis, fmt="e4m3"):
    dtype, down = {"e4m3": (ml_dtypes.float8_e4m3fn, 7), "e5m2": (ml_dtypes.float8_e5m2, 14)}[fmt]
    v = np.moveaxis(np.asarray(x, np.float32).astype(ml_dtypes.bfloat16).astype(np.float64), axis, -1)
    blocks = v.reshape(v.shape[:-1] + (-1, 32))
    amax = np.abs(blocks).max(-1, keepdims=True)
    byte = np.maximum(np.where(amax > 0, np.frexp(amax)[1] - 1 + 127, 0) - down, 1)
    scale = np.exp2(byte - 127.0)
    codes = (blocks / scale).astype(np.float32).astype(dtype).astype(np.float64)
    return np.moveaxis((codes * scale).reshape(v.shape), -1, axis)


WIDE = False


def mx_kscale(k):
    if not WIDE:
        return np.ones(k)
    levels = np.array([10, -10, 5, -5, 0])
    if k % 512:
        return np.exp2(np.random.permutation(np.resize(levels, k // 32))).repeat(32)
    a = np.empty((k // 512, 16))
    for p in range(k // 512):
        a[p, :8] = np.random.permutation(np.resize(levels, 8))
        for g in range(8):
            far = levels[np.abs(levels - a[p, g]) >= 10]
            a[p, g + 8] = far[np.random.randint(len(far))]
    return np.exp2(a.ravel()).repeat(32)


BF16 = ml_dtypes.bfloat16


def bf(x):
    return np.asarray(x, np.float32).astype(BF16)


def f64(x):
    return np.asarray(x).astype(np.float64)


N, D, E, G = 4096, 512, 1024, 3


def gained_product(left, right, p_row, q_row):
    return mxq(left * p_row[None, :], 1, "e4m3") @ mxq(q_row[:, None] * right, 0, "e4m3")


def mod_relu(z, b):
    return np.sign(z) * np.maximum(np.abs(z) + b[None, :], 0.0)


def draw0():
    cx = mx_kscale(E)
    c = np.stack([mx_kscale(D) for _ in range(G)])
    h = np.random.standard_normal((N, D))
    x = np.random.standard_normal((N, E)) * cx[None, :]
    a = np.random.standard_normal((D, D)) / np.sqrt(D)
    t = np.random.standard_normal((E, D)) / np.sqrt(E) / cx[:, None]
    p = (1.0 + 0.2 * np.random.standard_normal((G, D))) * c
    q = (1.0 + 0.2 * np.random.standard_normal((G, D))) / c
    b = np.random.uniform(-0.5, -0.1, D)
    return {"h": bf(h), "x": bf(x), "a": bf(a), "t": bf(t), "p": bf(p), "q": bf(q), "b": bf(b)}


def core(h, x, a, t, p, q, b):
    h, x, a, t, p, q, b = f64(h), f64(x), f64(a), f64(t), f64(p), f64(q), f64(b)
    s = a - a.T
    k1 = gained_product(h, s, p[0], q[0])
    s2 = gained_product(s, s, p[1], q[1])
    r = s / 2.0 + s2 / 6.0
    k23 = gained_product(k1, r, p[2], q[2])
    u = mxq(x, 1, "e4m3") @ mxq(t, 0, "e4m3")
    z = h + k1 + k23 + u
    return mod_relu(z, b)


def e4m3fn_bytes(y):
    return np.clip(np.asarray(y, np.float64), -448.0, 448.0).astype(np.float32).astype(ml_dtypes.float8_e4m3fn).view(np.uint8)


def e4m3fn_values(b):
    return np.asarray(b, np.uint8).view(ml_dtypes.float8_e4m3fn).astype(np.float64)


def setup_inputs():
    d = draw0()
    x0 = np.asarray(d['x']).astype(np.float64)
    s = (np.max(np.abs(x0), axis=(0,), keepdims=True) / 448.0).astype(np.float32)
    out = {}
    for k, v in d.items():
        if k == 'x':
            out['x_bytes'] = e4m3fn_bytes(x0 / s.astype(np.float64))
            out['x_scale'] = s
        else:
            out[k] = v
    return out


def reference(h, x_bytes, x_scale, a, t, p, q, b):
    return core(h, e4m3fn_values(x_bytes) * x_scale.astype(np.float64), a, t, p, q, b)

@@ -1,0 +1,358 @@
+from contextlib import ExitStack
+
+import concourse.mybir as mybir
+from concourse.masks import make_identity
+
+F32 = mybir.dt.float32
+BF16 = mybir.dt.bfloat16
+U32 = mybir.dt.uint32
+U8 = mybir.dt.uint8
+FP8 = mybir.dt.float8_e4m3fn
+FP8X4 = mybir.dt.float8_e4m3fn_x4
+ALU = mybir.AluOpType
+ACT = mybir.ActivationFunctionType
+
+N, D, E, G = 4096, 512, 1024, 3
+FLOPS = 2 * N * D * (2 * D + E) + 2 * D * D * D
+
+P = 128
+CHUNK = 512
+BLK = 256
+NB = N // BLK
+
+
+def tile_skewexptaylorrecurrentstep_t_kernel(tc, h, x_bytes, x_scale, a, t, p, q, b, out):
+    nc = tc.nc
+    h_v = h.rearrange("(i p j) k -> i p j k", p=P, j=4)
+    x_v = x_bytes.rearrange("(i p j) k -> i p j k", p=P, j=4)
+    o_v = out.rearrange("(i p j) k -> i p j k", p=P, j=4)
+
+    with ExitStack() as ctx:
+        keep = ctx.enter_context(tc.tile_pool(name="keep", bufs=1))
+        io = ctx.enter_context(tc.tile_pool(name="io", bufs=4))
+        sb = ctx.enter_context(tc.tile_pool(name="sb", bufs=3))
+        ps = ctx.enter_context(tc.psum_pool(name="ps", bufs=1))
+        ctx.enter_context(tc.manual_schedule())
+
+        x_in, h_in = {}, {}
+        xw, xt, ht, hq, xq, kq = {}, {}, {}, {}, {}, {}
+        hc, hs, xc, xs_, kc, ks = {}, {}, {}, {}, {}, {}
+        kt, kp, ki = {}, {}, {}
+        zp, zs, az, sg, ww = {}, {}, {}, {}, {}
+
+        def load(c):
+            xin = io.tile([P, 4, E], U8, name="xin", align_bytes=64)
+            nc.sync.dma_start(out=xin[:], in_=x_v[c])
+            hin = io.tile([P, 4, D], BF16, name="hin", align_bytes=64)
+            nc.sync.dma_start(out=hin[:], in_=h_v[c])
+            x_in[c] = xin
+            h_in[c] = hin
+
+        def cast(n):
+            w = sb.tile([P, 2, E], BF16, name="xw", align_bytes=64)
+            j0 = 2 * (n % 2)
+            nc.scalar.copy(out=w[:], in_=x_in[n // 2][:].bitcast(FP8)[:, j0 : j0 + 2, :])
+            xw[n] = w
+
+        def turn(n):
+            j0 = 2 * (n % 2)
+            hw = h_in[n // 2][:].bitcast(F32)
+            hb = ps.tile([P, 2, BLK], F32, name="ht")
+            for j in range(2):
+                for u in range(2):
+                    nc.tensor.transpose(hb[:, u, j * P : (j + 1) * P], hw[:, j0 + j, u::2], ident_f[:])
+            ht[n] = hb
+            ww_ = xw[n][:].bitcast(F32)
+            for g in range(2):
+                xb = ps.tile([P, 2, BLK], F32, name="xt", bufs=2)
+                for j in range(2):
+                    for u in range(2):
+                        nc.tensor.transpose(xb[:, u, j * P : (j + 1) * P], ww_[:, j, 256 * g + u : 256 * (g + 1) : 2], ident_f[:])
+                xt[n, g] = xb
+
+        def paired(bank):
+            return bank[:].bitcast(BF16).rearrange("p u (r e) -> p r u e", e=2)
+
+        def per_k(vec):
+            return vec.rearrange("p (u e) -> p u e", u=2).unsqueeze(1).to_broadcast([P, BLK, 2, 2])
+
+        def scale_h(n):
+            o = sb.tile([P, BLK, 4], BF16, name="hq", align_bytes=64)
+            nc.vector.tensor_tensor(
+                out=o[:].rearrange("p r (u e) -> p r u e", u=2), in0=paired(ht[n]), in1=per_k(pg[:, 0, :]), op=ALU.mult
+            )
+            hq[n] = o
+
+        def scale_x(n, g):
+            if g == 0:
+                o = sb.tile([P, 2, BLK, 4], BF16, name="xq", align_bytes=64)
+                xq[n] = o
+            nc.vector.tensor_tensor(
+                out=xq[n][:, g].rearrange("p r (u e) -> p r u e", u=2), in0=paired(xt[n, g]), in1=per_k(xsc[:, g, :]), op=ALU.mult
+            )
+
+        def quant_h(n):
+            c = sb.tile([P, BLK], U32, name="hc", bufs=4, align_bytes=64)
+            s = sb.tile([P, BLK], U8, name="hs", bufs=4, align_bytes=64)
+            nc.vector.quantize_mx(out=c[:].bitcast(FP8X4), scales=s[:], in_=hq[n][:].rearrange("p r t -> p (r t)"))
+            hc[n], hs[n] = c, s
+
+        def quant_x(n):
+            c = sb.tile([P, 2 * BLK], U32, name="xc", bufs=4, align_bytes=64)
+            s = sb.tile([P, 2 * BLK], U8, name="xs", bufs=4, align_bytes=64)
+            nc.vector.quantize_mx(out=c[:].bitcast(FP8X4), scales=s[:], in_=xq[n][:].rearrange("p g r t -> p (g r t)"))
+            xc[n], xs_[n] = c, s
+
+        def quant_k(n):
+            c = sb.tile([P, BLK], U32, name="kc", bufs=3, align_bytes=64)
+            s = sb.tile([P, BLK], U8, name="ks", bufs=3, align_bytes=64)
+            nc.vector.quantize_mx(out=c[:].bitcast(FP8X4), scales=s[:], in_=ki[n][:].rearrange("p r t -> p (r t)"))
+            kc[n], ks[n] = c, s
+
+        def k1t(n):
+            for half in range(2):
+                bank = ps.tile([P, 2, BLK], F32, name="kt", bufs=2)
+                for i in range(2):
+                    tt = 2 * half + i
+                    nc.tensor.matmul_mx(
+                        out=bank[:, i, :],
+                        lhsT=w0c[:, tt * P : (tt + 1) * P].bitcast(FP8X4),
+                        lhsT_scale=w0s[:, tt * P : (tt + 1) * P],
+                        rhs=hc[n][:].bitcast(FP8X4),
+                        rhs_scale=hs[n][:],
+                        start=True,
+                        stop=True,
+                    )
+                kt[n, half] = bank
+
+        def planes(n):
+            o = sb.tile([P, 4, BLK], BF16, name="kp", bufs=2, align_bytes=64)
+            for tt in range(4):
+                nc.scalar.activation(out=o[:, tt, :], in_=kt[n, tt // 2][:, tt % 2, :], func=ACT.Copy, scale=p2f[:, tt : tt + 1])
+            kp[n] = o
+
+        def weave(n):
+            bank = ps.tile([P, BLK, 4], BF16, name="kb")
+            for half in range(2):
+                cols = slice(half * P, (half + 1) * P)
+                nc.tensor.matmul(
+                    out=bank[:, cols, :].rearrange("p r t -> p (r t)"),
+                    lhsT=ident_b[:],
+                    rhs=kp[n][:, :, cols].rearrange("p t r -> p r t"),
+                    start=True,
+                    stop=True,
+                )
+            kq[n] = bank
+
+        def k_out(n):
+            o = sb.tile([P, BLK, 4], BF16, name="ki", bufs=2, align_bytes=64)
+            nc.scalar.copy(out=o[:], in_=kq[n][:])
+            ki[n] = o
+
+        def z_sum(n, j):
+            bank = ps.tile([P, D], F32, name="zb", bufs=2)
+            cols = slice(j * P, (j + 1) * P)
+            cols1 = slice(BLK + j * P, BLK + (j + 1) * P)
+            left = [(hc[n][:, cols], hs[n][:, cols]), (xc[n][:, cols], xs_[n][:, cols]), (xc[n][:, cols1], xs_[n][:, cols1]), (kc[n][:, cols], ks[n][:, cols])]
+            right = [(w0c[:], w0s[:]), (tc_[:, 0, :], ts_[:, 0, :]), (tc_[:, 1, :], ts_[:, 1, :]), (w2c[:], w2s[:])]
+            for i in range(4):
+                nc.tensor.matmul_mx(
+                    out=bank[:],
+                    lhsT=left[i][0].bitcast(FP8X4),
+                    lhsT_scale=left[i][1],
+                    rhs=right[i][0].bitcast(FP8X4),
+                    rhs_scale=right[i][1],
+                    start=(i == 0),
+                    stop=(i == 3),
+                )
+            zp[n, j] = bank
+
+        def z_out(n, j):
+            if j == 0:
+                o = sb.tile([P, 2, D], F32, name="zs", align_bytes=64)
+                zs[n] = o
+            nc.vector.tensor_tensor(
+                out=zs[n][:, j, :].rearrange("p (m t) -> p m t", t=4),
+                in0=zp[n, j][:].rearrange("p (t m) -> p m t", t=4),
+                in1=h_in[n // 2][:, 2 * (n % 2) + j, :].rearrange("p (m t) -> p m t", t=4),
+                op=ALU.add,
+            )
+
+        def mag(n):
+            o = sb.tile([P, 2, D], F32, name="az", bufs=2, align_bytes=64)
+            nc.scalar.activation(out=o[:], in_=zs[n][:], func=ACT.Abs)
+            az[n] = o
+
+        def sign(n):
+            o = sb.tile([P, 2, D], BF16, name="sg", bufs=2, align_bytes=64)
+            nc.scalar.activation(out=o[:], in_=zs[n][:], func=ACT.Sign)
+            sg[n] = o
+
+        def add_b(n):
+            o = sb.tile([P, 2, D], F32, name="wb", bufs=2, align_bytes=64)
+            nc.gpsimd.tensor_tensor(out=o[:], in0=az[n][:], in1=bias[:].unsqueeze(1).to_broadcast([P, 2, D]), op=ALU.add)
+            ww[n] = o
+
+        def finish(n):
+            o = sb.tile([P, 2, D], F32, name="res", align_bytes=64)
+            nc.vector.scalar_tensor_tensor(out=o[:], in0=ww[n][:], scalar=0.0, in1=sg[n][:], op0=ALU.max, op1=ALU.mult)
+            j0 = 2 * (n % 2)
+            nc.sync.dma_start(out=o_v[n // 2][:, j0 : j0 + 2, :], in_=o[:])
+
+        a4 = keep.tile([P, 4, D], BF16, name="a4", align_bytes=64)
+        nc.sync.dma_start(out=a4[:], in_=a.rearrange("(p j) n -> p j n", j=4))
+        pg = keep.tile([P, 3, 4], BF16, name="pg", align_bytes=64)
+        nc.scalar.dma_start(out=pg[:], in_=p.rearrange("g (p t) -> p g t", t=4))
+        qg = keep.tile([P, 3, 4], BF16, name="qg", align_bytes=64)
+        nc.scalar.dma_start(out=qg[:], in_=q.rearrange("g (p t) -> p g t", t=4))
+        xsc = keep.tile([P, 2, 4], F32, name="xsc", align_bytes=64)
+        nc.scalar.dma_start(out=xsc[:], in_=x_scale.rearrange("o (g p t) -> p (o g) t", p=P, t=4))
+        ident_f = keep.tile([P, P], F32, name="ident_f", align_bytes=64)
+        make_identity(nc, ident_f[:])
+        ident_b = keep.tile([P, P], BF16, name="ident_b", align_bytes=64)
+        make_identity(nc, ident_b[:])
+        load(0)
+        t4 = keep.tile([P, 2, 4, D], BF16, name="t4", align_bytes=64)
+        nc.sync.dma_start(out=t4[:], in_=t.rearrange("(g p j) n -> p g j n", p=P, j=4))
+        bias = keep.tile([P, D], BF16, name="bias", align_bytes=64)
+        nc.sync.dma_start(out=bias[:], in_=b.partition_broadcast(P))
+        load(1)
+        load(2)
+
+        p2f = keep.tile([P, 4], F32, name="p2f", align_bytes=64)
+        nc.vector.tensor_copy(out=p2f[:], in_=pg[:, 2, :])
+        p1n = keep.tile([P, 4], F32, name="p1n", align_bytes=64)
+        nc.vector.tensor_scalar(out=p1n[:], in0=pg[:, 1, :], scalar1=-1.0, scalar2=None, op0=ALU.mult)
+        q2h = keep.tile([P, 4], F32, name="q2h", align_bytes=64)
+        nc.vector.tensor_scalar(out=q2h[:], in0=qg[:, 2, :], scalar1=0.5, scalar2=None, op0=ALU.mult)
+
+        def kscale(vec, cols):
+            return vec.unsqueeze(1).to_broadcast([P, cols, 4])
+
+        s_f = keep.tile([P, D, 4], F32, name="s_f", align_bytes=64)
+        aw = a4[:].bitcast(F32)
+        a_v = a4[:].rearrange("p (u e) (m j) -> p j m u e", u=2, j=4)
+        for jj in range(2):
+            bank = ps.tile([P, 2, 2, P], F32, name="zb", bufs=2)
+            for i in range(2):
+                for u in range(2):
+                    nc.tensor.transpose(bank[:, i, u, :], aw[:, 2 * jj + i, u::2], ident_f[:])
+            for i in range(2):
+                j = 2 * jj + i
+                nc.vector.tensor_tensor(
+                    out=s_f[:, j * P : (j + 1) * P, :].rearrange("p m (u e) -> p m u e", u=2),
+                    in0=a_v[:, j],
+                    in1=bank[:, i].bitcast(BF16).rearrange("p u (m e) -> p m u e", e=2),
+                    op=ALU.subtract,
+                )
+
+        def quant_w(src, name):
+            c = keep.tile([P, D], U32, name=name + "c", align_bytes=64)
+            s = keep.tile([P, D], U8, name=name + "s", align_bytes=64)
+            nc.vector.quantize_mx(out=c[:].bitcast(FP8X4), scales=s[:], in_=src[:].rearrange("p c t -> p (c t)"))
+            return c, s
+
+        cast(0)
+        turn(0)
+        cast(1)
+        p1s = keep.tile([P, D, 4], BF16, name="p1s", align_bytes=64)
+        nc.gpsimd.tensor_tensor(out=p1s[:], in0=s_f[:], in1=kscale(p1n[:], D), op=ALU.mult)
+        q0s = keep.tile([P, D, 4], BF16, name="q0s", align_bytes=64)
+        nc.vector.tensor_tensor(out=q0s[:], in0=s_f[:], in1=kscale(qg[:, 0, :], D), op=ALU.mult)
+        q1s = keep.tile([P, D, 4], BF16, name="q1s", align_bytes=64)
+        nc.gpsimd.tensor_tensor(out=q1s[:], in0=s_f[:], in1=kscale(qg[:, 1, :], D), op=ALU.mult)
+        w0c, w0s = quant_w(q0s, "w0")
+        scale_h(0)
+        scale_x(0, 0)
+        scale_x(0, 1)
+        quant_h(0)
+        quant_x(0)
+        turn(1)
+
+        tg = keep.tile([P, 2, D, 4], BF16, name="tg", align_bytes=64)
+        tc_ = keep.tile([P, 2, D], U32, name="tc", align_bytes=64)
+        ts_ = keep.tile([P, 2, D], U8, name="ts", align_bytes=64)
+        for g in range(2):
+            nc.scalar.copy(
+                out=tg[:, g].rearrange("p (t m) j -> p t m j", t=4), in_=t4[:, g].rearrange("p j (m t) -> p t m j", t=4)
+            )
+
+        k1t(0)
+        planes(0)
+        scale_h(1)
+        scale_x(1, 0)
+        scale_x(1, 1)
+        quant_h(1)
+        quant_x(1)
+        weave(0)
+        k_out(0)
+        cast(2)
+        turn(2)
+        lc, ls = quant_w(p1s, "l1")
+        rc, rs = quant_w(q1s, "r1")
+        for g in range(2):
+            nc.vector.quantize_mx(out=tc_[:, g, :].bitcast(FP8X4), scales=ts_[:, g, :], in_=tg[:, g].rearrange("p c t -> p (c t)"))
+        quant_k(0)
+        r_f = keep.tile([P, D, 4], F32, name="r_f", align_bytes=64)
+        for cq in range(4):
+            cols = slice(cq * P, (cq + 1) * P)
+            bank = ps.tile([P, 4, P], F32, name="zb", bufs=2)
+            for tt in range(4):
+                nc.tensor.matmul_mx(
+                    out=bank[:, tt, :],
+                    lhsT=lc[:, tt * P : (tt + 1) * P].bitcast(FP8X4),
+                    lhsT_scale=ls[:, tt * P : (tt + 1) * P],
+                    rhs=rc[:, cols].bitcast(FP8X4),
+                    rhs_scale=rs[:, cols],
+                    start=True,
+                    stop=True,
+                )
+            nc.vector.scalar_tensor_tensor(
+                out=r_f[:, cols, :],
+                in0=bank[:].rearrange("p t c -> p c t"),
+                scalar=1.0 / 3.0,
+                in1=s_f[:, cols, :],
+                op0=ALU.mult,
+                op1=ALU.add,
+            )
+        q2r = keep.tile([P, D, 4], BF16, name="q2r", align_bytes=64)
+        nc.vector.tensor_tensor(out=q2r[:], in0=r_f[:], in1=kscale(q2h[:], D), op=ALU.mult)
+        w2c, w2s = quant_w(q2r, "w2")
+        cast(3)
+
+        for n in range(1, NB + 2):
+            if n % 2 == 0 and (n + 4) // 2 < NB // 2:
+                load((n + 4) // 2)
+            if n < NB:
+                k1t(n)
+            if n - 1 < NB:
+                for j in range(2):
+                    z_sum(n - 1, j)
+            if n + 1 < NB:
+                scale_h(n + 1)
+                scale_x(n + 1, 0)
+                scale_x(n + 1, 1)
+            if n >= 2:
+                mag(n - 2)
+            if n < NB:
+                planes(n)
+            if n >= 2:
+                add_b(n - 2)
+                sign(n - 2)
+            if n - 1 < NB:
+                for j in range(2):
+                    z_out(n - 1, j)
+            if n < NB:
+                weave(n)
+                k_out(n)
+            if n + 1 < NB:
+                quant_h(n + 1)
+                quant_x(n + 1)
+            if n < NB:
+                quant_k(n)
+            if n >= 2:
+                finish(n - 2)
+            if n + 3 < NB:
+                cast(n + 3)
+            if n + 2 < NB:
+                turn(n + 2)

@@ -35,10 +35,10 @@ def tile_skewexptaylorrecurrentstep_t_kernel(tc, h, x_bytes, x_scale, a, t, p, q
         ctx.enter_context(tc.manual_schedule())
 
         x_in, h_in = {}, {}
-        xw, xt, ht, hq, xq, kq = {}, {}, {}, {}, {}, {}
-        hc, hs, xc, xs_, kc, ks = {}, {}, {}, {}, {}, {}
-        kt, kp, ki = {}, {}, {}
-        zp, zs, az, sg, ww = {}, {}, {}, {}, {}
+        xw, xt, ht, kq = {}, {}, {}, {}
+        qin, codes = {}, {}
+        kt, kp = {}, {}
+        zp, zs, az, sg, ww, rs_ = {}, {}, {}, {}, {}, {}
 
         def load(c):
             xin = io.tile([P, 4, E], U8, name="xin", align_bytes=64)
@@ -54,7 +54,7 @@ def tile_skewexptaylorrecurrentstep_t_kernel(tc, h, x_bytes, x_scale, a, t, p, q
             nc.scalar.copy(out=w[:], in_=x_in[n // 2][:].bitcast(FP8)[:, j0 : j0 + 2, :])
             xw[n] = w
 
-        def turn(n):
+        def turn_h(n):
             j0 = 2 * (n % 2)
             hw = h_in[n // 2][:].bitcast(F32)
             hb = ps.tile([P, 2, BLK], F32, name="ht")
@@ -62,6 +62,8 @@ def tile_skewexptaylorrecurrentstep_t_kernel(tc, h, x_bytes, x_scale, a, t, p, q
                 for u in range(2):
                     nc.tensor.transpose(hb[:, u, j * P : (j + 1) * P], hw[:, j0 + j, u::2], ident_f[:])
             ht[n] = hb
+
+        def turn_x(n):
             ww_ = xw[n][:].bitcast(F32)
             for g in range(2):
                 xb = ps.tile([P, 2, BLK], F32, name="xt", bufs=2)
@@ -76,38 +78,37 @@ def tile_skewexptaylorrecurrentstep_t_kernel(tc, h, x_bytes, x_scale, a, t, p, q
         def per_k(vec):
             return vec.rearrange("p (u e) -> p u e", u=2).unsqueeze(1).to_broadcast([P, BLK, 2, 2])
 
+        def stage(n):
+            if n not in qin:
+                tile = sb.tile([P, 4, BLK, 4], BF16, name="qin", align_bytes=64)
+                qin[n] = tile
+            return qin[n]
+
         def scale_h(n):
-            o = sb.tile([P, BLK, 4], BF16, name="hq", align_bytes=64)
             nc.vector.tensor_tensor(
-                out=o[:].rearrange("p r (u e) -> p r u e", u=2), in0=paired(ht[n]), in1=per_k(pg[:, 0, :]), op=ALU.mult
+                out=stage(n - 1)[:, 2].rearrange("p r (u e) -> p r u e", u=2), in0=paired(ht[n]), in1=per_k(pg[:, 0, :]), op=ALU.mult
             )
-            hq[n] = o
 
         def scale_x(n, g):
-            if g == 0:
-                o = sb.tile([P, 2, BLK, 4], BF16, name="xq", align_bytes=64)
-                xq[n] = o
             nc.vector.tensor_tensor(
-                out=xq[n][:, g].rearrange("p r (u e) -> p r u e", u=2), in0=paired(xt[n, g]), in1=per_k(xsc[:, g, :]), op=ALU.mult
+                out=stage(n)[:, g].rearrange("p r (u e) -> p r u e", u=2), in0=paired(xt[n, g]), in1=per_k(xsc[:, g, :]), op=ALU.mult
             )
 
-        def quant_h(n):
-            c = sb.tile([P, BLK], U32, name="hc", bufs=4, align_bytes=64)
-            s = sb.tile([P, BLK], U8, name="hs", bufs=4, align_bytes=64)
-            nc.vector.quantize_mx(out=c[:].bitcast(FP8X4), scales=s[:], in_=hq[n][:].rearrange("p r t -> p (r t)"))
-            hc[n], hs[n] = c, s
+        def quant(n, lo=0, hi=4):
+            if n not in codes:
+                c = sb.tile([P, 4, BLK], U32, name="codes", bufs=5, align_bytes=64)
+                sc = sb.tile([P, 4, BLK], U8, name="scales", bufs=5, align_bytes=64)
+                codes[n] = (c, sc)
+            c, sc = codes[n]
+            nc.vector.quantize_mx(
+                out=c[:, lo:hi].rearrange("p o r -> p (o r)").bitcast(FP8X4),
+                scales=sc[:, lo:hi].rearrange("p o r -> p (o r)"),
+                in_=qin[n][:, lo:hi].rearrange("p o r t -> p (o r t)"),
+            )
 
-        def quant_x(n):
-            c = sb.tile([P, 2 * BLK], U32, name="xc", bufs=4, align_bytes=64)
-            s = sb.tile([P, 2 * BLK], U8, name="xs", bufs=4, align_bytes=64)
-            nc.vector.quantize_mx(out=c[:].bitcast(FP8X4), scales=s[:], in_=xq[n][:].rearrange("p g r t -> p (g r t)"))
-            xc[n], xs_[n] = c, s
-
-        def quant_k(n):
-            c = sb.tile([P, BLK], U32, name="kc", bufs=3, align_bytes=64)
-            s = sb.tile([P, BLK], U8, name="ks", bufs=3, align_bytes=64)
-            nc.vector.quantize_mx(out=c[:].bitcast(FP8X4), scales=s[:], in_=ki[n][:].rearrange("p r t -> p (r t)"))
-            kc[n], ks[n] = c, s
+        def part(n, o, cols):
+            c, sc = codes[n - 1 if o == 2 else n]
+            return c[:, o, cols].bitcast(FP8X4), sc[:, o, cols]
 
         def k1t(n):
             for half in range(2):
@@ -118,8 +119,8 @@ def tile_skewexptaylorrecurrentstep_t_kernel(tc, h, x_bytes, x_scale, a, t, p, q
                         out=bank[:, i, :],
                         lhsT=w0c[:, tt * P : (tt + 1) * P].bitcast(FP8X4),
                         lhsT_scale=w0s[:, tt * P : (tt + 1) * P],
-                        rhs=hc[n][:].bitcast(FP8X4),
-                        rhs_scale=hs[n][:],
+                        rhs=part(n, 2, slice(0, BLK))[0],
+                        rhs_scale=part(n, 2, slice(0, BLK))[1],
                         start=True,
                         stop=True,
                     )
@@ -145,20 +146,17 @@ def tile_skewexptaylorrecurrentstep_t_kernel(tc, h, x_bytes, x_scale, a, t, p, q
             kq[n] = bank
 
         def k_out(n):
-            o = sb.tile([P, BLK, 4], BF16, name="ki", bufs=2, align_bytes=64)
-            nc.scalar.copy(out=o[:], in_=kq[n][:])
-            ki[n] = o
+            nc.scalar.copy(out=stage(n)[:, 3], in_=kq[n][:])
 
         def z_sum(n, j):
             bank = ps.tile([P, D], F32, name="zb", bufs=2)
             cols = slice(j * P, (j + 1) * P)
-            cols1 = slice(BLK + j * P, BLK + (j + 1) * P)
-            left = [(hc[n][:, cols], hs[n][:, cols]), (xc[n][:, cols], xs_[n][:, cols]), (xc[n][:, cols1], xs_[n][:, cols1]), (kc[n][:, cols], ks[n][:, cols])]
+            left = [part(n, 2, cols), part(n, 0, cols), part(n, 1, cols), part(n, 3, cols)]
             right = [(w0c[:], w0s[:]), (tc_[:, 0, :], ts_[:, 0, :]), (tc_[:, 1, :], ts_[:, 1, :]), (w2c[:], w2s[:])]
             for i in range(4):
                 nc.tensor.matmul_mx(
                     out=bank[:],
-                    lhsT=left[i][0].bitcast(FP8X4),
+                    lhsT=left[i][0],
                     lhsT_scale=left[i][1],
                     rhs=right[i][0].bitcast(FP8X4),
                     rhs_scale=right[i][1],
@@ -168,7 +166,7 @@ def tile_skewexptaylorrecurrentstep_t_kernel(tc, h, x_bytes, x_scale, a, t, p, q
             zp[n, j] = bank
 
         def z_out(n, j):
-            if j == 0:
+            if n not in zs:
                 o = sb.tile([P, 2, D], F32, name="zs", align_bytes=64)
                 zs[n] = o
             nc.vector.tensor_tensor(
@@ -178,73 +176,48 @@ def tile_skewexptaylorrecurrentstep_t_kernel(tc, h, x_bytes, x_scale, a, t, p, q
                 op=ALU.add,
             )
 
-        def mag(n):
-            o = sb.tile([P, 2, D], F32, name="az", bufs=2, align_bytes=64)
-            nc.scalar.activation(out=o[:], in_=zs[n][:], func=ACT.Abs)
-            az[n] = o
+        def mag(n, js):
+            if n not in az:
+                o = sb.tile([P, 2, D], F32, name="az", bufs=2, align_bytes=64)
+                az[n] = o
+            nc.scalar.activation(out=az[n][:, js], in_=zs[n][:, js], func=ACT.Abs)
 
-        def sign(n):
-            o = sb.tile([P, 2, D], BF16, name="sg", bufs=2, align_bytes=64)
-            nc.scalar.activation(out=o[:], in_=zs[n][:], func=ACT.Sign)
-            sg[n] = o
+        def sign(n, js):
+            if n not in sg:
+                o = sb.tile([P, 2, D], BF16, name="sg", bufs=2, align_bytes=64)
+                sg[n] = o
+            nc.scalar.activation(out=sg[n][:, js], in_=zs[n][:, js], func=ACT.Sign)
 
-        def add_b(n):
-            o = sb.tile([P, 2, D], F32, name="wb", bufs=2, align_bytes=64)
-            nc.gpsimd.tensor_tensor(out=o[:], in0=az[n][:], in1=bias[:].unsqueeze(1).to_broadcast([P, 2, D]), op=ALU.add)
-            ww[n] = o
+        def add_b(n, js, eng):
+            if n not in ww:
+                o = sb.tile([P, 2, D], F32, name="wb", bufs=2, align_bytes=64)
+                ww[n] = o
+            cnt = js.stop - js.start
+            eng.tensor_tensor(out=ww[n][:, js], in0=az[n][:, js], in1=bias[:].unsqueeze(1).to_broadcast([P, cnt, D]), op=ALU.add)
 
-        def finish(n):
-            o = sb.tile([P, 2, D], F32, name="res", align_bytes=64)
-            nc.vector.scalar_tensor_tensor(out=o[:], in0=ww[n][:], scalar=0.0, in1=sg[n][:], op0=ALU.max, op1=ALU.mult)
+        def finish(n, js):
+            if n not in rs_:
+                o = sb.tile([P, 2, D], F32, name="res", align_bytes=64)
+                rs_[n] = o
+            nc.vector.scalar_tensor_tensor(out=rs_[n][:, js], in0=ww[n][:, js], scalar=0.0, in1=sg[n][:, js], op0=ALU.max, op1=ALU.mult)
             j0 = 2 * (n % 2)
-            nc.sync.dma_start(out=o_v[n // 2][:, j0 : j0 + 2, :], in_=o[:])
+            nc.sync.dma_start(out=o_v[n // 2][:, j0 + js.start : j0 + js.stop, :], in_=rs_[n][:, js])
 
+        both = slice(0, 2)
         a4 = keep.tile([P, 4, D], BF16, name="a4", align_bytes=64)
-        nc.sync.dma_start(out=a4[:], in_=a.rearrange("(p j) n -> p j n", j=4))
         pg = keep.tile([P, 3, 4], BF16, name="pg", align_bytes=64)
-        nc.scalar.dma_start(out=pg[:], in_=p.rearrange("g (p t) -> p g t", t=4))
         qg = keep.tile([P, 3, 4], BF16, name="qg", align_bytes=64)
-        nc.scalar.dma_start(out=qg[:], in_=q.rearrange("g (p t) -> p g t", t=4))
         xsc = keep.tile([P, 2, 4], F32, name="xsc", align_bytes=64)
-        nc.scalar.dma_start(out=xsc[:], in_=x_scale.rearrange("o (g p t) -> p (o g) t", p=P, t=4))
-        ident_f = keep.tile([P, P], F32, name="ident_f", align_bytes=64)
-        make_identity(nc, ident_f[:])
         ident_b = keep.tile([P, P], BF16, name="ident_b", align_bytes=64)
-        make_identity(nc, ident_b[:])
-        load(0)
+        ident_f = keep.tile([P, P], F32, name="ident_f", align_bytes=64)
+        neg_b = keep.tile([P, P], BF16, name="neg_b", align_bytes=64)
         t4 = keep.tile([P, 2, 4, D], BF16, name="t4", align_bytes=64)
-        nc.sync.dma_start(out=t4[:], in_=t.rearrange("(g p j) n -> p g j n", p=P, j=4))
         bias = keep.tile([P, D], BF16, name="bias", align_bytes=64)
-        nc.sync.dma_start(out=bias[:], in_=b.partition_broadcast(P))
-        load(1)
-        load(2)
-
-        p2f = keep.tile([P, 4], F32, name="p2f", align_bytes=64)
-        nc.vector.tensor_copy(out=p2f[:], in_=pg[:, 2, :])
         p1n = keep.tile([P, 4], F32, name="p1n", align_bytes=64)
-        nc.vector.tensor_scalar(out=p1n[:], in0=pg[:, 1, :], scalar1=-1.0, scalar2=None, op0=ALU.mult)
+        p2f = keep.tile([P, 4], F32, name="p2f", align_bytes=64)
         q2h = keep.tile([P, 4], F32, name="q2h", align_bytes=64)
-        nc.vector.tensor_scalar(out=q2h[:], in0=qg[:, 2, :], scalar1=0.5, scalar2=None, op0=ALU.mult)
-
         def kscale(vec, cols):
             return vec.unsqueeze(1).to_broadcast([P, cols, 4])
-
-        s_f = keep.tile([P, D, 4], F32, name="s_f", align_bytes=64)
-        aw = a4[:].bitcast(F32)
-        a_v = a4[:].rearrange("p (u e) (m j) -> p j m u e", u=2, j=4)
-        for jj in range(2):
-            bank = ps.tile([P, 2, 2, P], F32, name="zb", bufs=2)
-            for i in range(2):
-                for u in range(2):
-                    nc.tensor.transpose(bank[:, i, u, :], aw[:, 2 * jj + i, u::2], ident_f[:])
-            for i in range(2):
-                j = 2 * jj + i
-                nc.vector.tensor_tensor(
-                    out=s_f[:, j * P : (j + 1) * P, :].rearrange("p m (u e) -> p m u e", u=2),
-                    in0=a_v[:, j],
-                    in1=bank[:, i].bitcast(BF16).rearrange("p u (m e) -> p m u e", e=2),
-                    op=ALU.subtract,
-                )
 
         def quant_w(src, name):
             c = keep.tile([P, D], U32, name=name + "c", align_bytes=64)
@@ -252,51 +225,51 @@ def tile_skewexptaylorrecurrentstep_t_kernel(tc, h, x_bytes, x_scale, a, t, p, q
             nc.vector.quantize_mx(out=c[:].bitcast(FP8X4), scales=s[:], in_=src[:].rearrange("p c t -> p (c t)"))
             return c, s
 
-        cast(0)
-        turn(0)
-        cast(1)
-        p1s = keep.tile([P, D, 4], BF16, name="p1s", align_bytes=64)
-        nc.gpsimd.tensor_tensor(out=p1s[:], in0=s_f[:], in1=kscale(p1n[:], D), op=ALU.mult)
+        s_f = keep.tile([P, D, 4], F32, name="s_f", align_bytes=64)
         q0s = keep.tile([P, D, 4], BF16, name="q0s", align_bytes=64)
-        nc.vector.tensor_tensor(out=q0s[:], in0=s_f[:], in1=kscale(qg[:, 0, :], D), op=ALU.mult)
-        q1s = keep.tile([P, D, 4], BF16, name="q1s", align_bytes=64)
-        nc.gpsimd.tensor_tensor(out=q1s[:], in0=s_f[:], in1=kscale(qg[:, 1, :], D), op=ALU.mult)
-        w0c, w0s = quant_w(q0s, "w0")
-        scale_h(0)
-        scale_x(0, 0)
-        scale_x(0, 1)
-        quant_h(0)
-        quant_x(0)
-        turn(1)
+        sbank = {}
+        def skew(cq):
+            bank = ps.tile([P, 4, P], F32, name="sbank", tag=("zb", "xt")[cq // 2], bufs=2)
+            for tt in range(4):
+                nc.tensor.matmul(out=bank[:, tt, :], lhsT=ident_b[:], rhs=a4[:, tt, cq::4], start=True, stop=False)
+                nc.tensor.matmul(out=bank[:, tt, :], lhsT=a4[:, cq, tt::4], rhs=neg_b[:], start=False, stop=True)
+            sbank[cq] = bank
 
+        def gain_q0(cq):
+            cols = slice(cq * P, (cq + 1) * P)
+            nc.vector.tensor_tensor(out=q0s[:, cols], in0=sbank[cq][:].rearrange("p t c -> p c t"), in1=kscale(qg[:, 0, :], P), op=ALU.mult)
+
+        def keep_s(cq):
+            cols = slice(cq * P, (cq + 1) * P)
+            nc.scalar.copy(out=s_f[:, cols], in_=sbank[cq][:].rearrange("p t c -> p c t"))
+
+        p1s = keep.tile([P, D, 4], BF16, name="p1s", align_bytes=64)
+        q1s = keep.tile([P, D, 4], BF16, name="q1s", align_bytes=64)
         tg = keep.tile([P, 2, D, 4], BF16, name="tg", align_bytes=64)
         tc_ = keep.tile([P, 2, D], U32, name="tc", align_bytes=64)
         ts_ = keep.tile([P, 2, D], U8, name="ts", align_bytes=64)
-        for g in range(2):
-            nc.scalar.copy(
-                out=tg[:, g].rearrange("p (t m) j -> p t m j", t=4), in_=t4[:, g].rearrange("p j (m t) -> p t m j", t=4)
-            )
-
-        k1t(0)
-        planes(0)
-        scale_h(1)
-        scale_x(1, 0)
-        scale_x(1, 1)
-        quant_h(1)
-        quant_x(1)
-        weave(0)
-        k_out(0)
-        cast(2)
-        turn(2)
-        lc, ls = quant_w(p1s, "l1")
-        rc, rs = quant_w(q1s, "r1")
-        for g in range(2):
-            nc.vector.quantize_mx(out=tc_[:, g, :].bitcast(FP8X4), scales=ts_[:, g, :], in_=tg[:, g].rearrange("p c t -> p (c t)"))
-        quant_k(0)
         r_f = keep.tile([P, D, 4], F32, name="r_f", align_bytes=64)
-        for cq in range(4):
+        q2r = keep.tile([P, D, 4], BF16, name="q2r", align_bytes=64)
+        def gain_q1(cq):
             cols = slice(cq * P, (cq + 1) * P)
-            bank = ps.tile([P, 4, P], F32, name="zb", bufs=2)
+            nc.gpsimd.tensor_tensor(out=q1s[:, cols], in0=s_f[:, cols], in1=kscale(qg[:, 1, :], P), op=ALU.mult)
+
+        def weave_t(g, half):
+            bank = ps.tile([P, BLK, 4], BF16, name="tb", tag=("kb", "zb")[half], bufs=(1, 2)[half])
+            for i in range(2):
+                cq = 2 * half + i
+                nc.tensor.matmul(
+                    out=bank[:, i * P : (i + 1) * P, :].rearrange("p m j -> p (m j)"),
+                    lhsT=ident_b[:],
+                    rhs=t4[:, g, :, cq::4].rearrange("p j m -> p m j"),
+                    start=True,
+                    stop=True,
+                )
+            nc.scalar.copy(out=tg[:, g, half * BLK : (half + 1) * BLK, :], in_=bank[:])
+
+        def square(cq):
+            cols = slice(cq * P, (cq + 1) * P)
+            bank = ps.tile([P, 4, P], F32, name="s2", tag="zb", bufs=2)
             for tt in range(4):
                 nc.tensor.matmul_mx(
                     out=bank[:, tt, :],
@@ -307,52 +280,200 @@ def tile_skewexptaylorrecurrentstep_t_kernel(tc, h, x_bytes, x_scale, a, t, p, q
                     start=True,
                     stop=True,
                 )
+            sq[cq] = bank
+
+        def series(cq):
+            cols = slice(cq * P, (cq + 1) * P)
             nc.vector.scalar_tensor_tensor(
                 out=r_f[:, cols, :],
-                in0=bank[:].rearrange("p t c -> p c t"),
+                in0=sq[cq][:].rearrange("p t c -> p c t"),
                 scalar=1.0 / 3.0,
                 in1=s_f[:, cols, :],
                 op0=ALU.mult,
                 op1=ALU.add,
             )
-        q2r = keep.tile([P, D, 4], BF16, name="q2r", align_bytes=64)
-        nc.vector.tensor_tensor(out=q2r[:], in0=r_f[:], in1=kscale(q2h[:], D), op=ALU.mult)
-        w2c, w2s = quant_w(q2r, "w2")
-        cast(3)
 
-        for n in range(1, NB + 2):
-            if n % 2 == 0 and (n + 4) // 2 < NB // 2:
+        sq = {}
+        def gain_r(cq):
+            cols = slice(cq * P, (cq + 1) * P)
+            nc.gpsimd.tensor_tensor(out=q2r[:, cols], in0=r_f[:, cols], in1=kscale(q2h[:], P), op=ALU.mult)
+
+        def gain_v(cq):
+            cols = slice(cq * P, (cq + 1) * P)
+            nc.vector.tensor_tensor(out=p1s[:, cols], in0=sbank[cq][:].rearrange("p t c -> p c t"), in1=kscale(p1n[:], P), op=ALU.mult)
+
+        def quant_t(g):
+            nc.vector.quantize_mx(out=tc_[:, g, :].bitcast(FP8X4), scales=ts_[:, g, :], in_=tg[:, g].rearrange("p c t -> p (c t)"))
+
+        one = slice(0, 1)
+        two = slice(1, 2)
+
+        make_identity(nc, ident_b[:])
+        nc.sync.dma_start(out=a4[:], in_=a.rearrange("(p j) n -> p j n", j=4))
+        nc.vector.tensor_scalar(out=neg_b[:], in0=ident_b[:], scalar1=-1.0, scalar2=None, op0=ALU.mult)
+        nc.scalar.dma_start(out=pg[:], in_=p.rearrange("g (p t) -> p g t", t=4))
+        nc.scalar.dma_start(out=qg[:], in_=q.rearrange("g (p t) -> p g t", t=4))
+        nc.scalar.dma_start(out=xsc[:], in_=x_scale.rearrange("o (g p t) -> p (o g) t", p=P, t=4))
+        nc.vector.tensor_scalar(out=p1n[:], in0=pg[:, 1, :], scalar1=-1.0, scalar2=None, op0=ALU.mult)
+        load(0)
+        skew(2)
+        nc.vector.tensor_copy(out=p2f[:], in_=pg[:, 2, :])
+        skew(0)
+        gain_q0(2)
+        skew(1)
+        gain_q0(0)
+        keep_s(2)
+        gain_q0(1)
+        nc.sync.dma_start(out=t4[:], in_=t.rearrange("(g p j) n -> p g j n", p=P, j=4))
+        make_identity(nc, ident_f[:])
+        keep_s(0)
+        skew(3)
+        turn_h(0)
+        gain_v(2)
+        keep_s(1)
+        scale_h(0)
+        turn_h(1)
+        gain_q0(3)
+        keep_s(3)
+        quant(-1, 2, 3)
+        gain_q1(2)
+        w0c, w0s = quant_w(q0s, "w0")
+        gain_v(3)
+        nc.sync.dma_start(out=bias[:], in_=b.partition_broadcast(P))
+        cast(0)
+        gain_q1(1)
+        k1t(0)
+        gain_q1(3)
+        gain_q1(0)
+        turn_x(0)
+        planes(0)
+        weave(0)
+        gain_v(1)
+        gain_v(0)
+        scale_h(1)
+        nc.vector.tensor_scalar(out=q2h[:], in0=qg[:, 2, :], scalar1=0.5, scalar2=None, op0=ALU.mult)
+        lc, ls = quant_w(p1s, "l1")
+        rc, rs = quant_w(q1s, "r1")
+        scale_x(0, 0)
+        square(1)
+        square(0)
+        series(0)
+        cast(1)
+        series(1)
+        load(1)
+        turn_h(2)
+        k_out(0)
+        square(2)
+        scale_x(0, 1)
+        cast(2)
+        weave_t(0, 0)
+        series(2)
+        load(2)
+        square(3)
+        gain_r(0)
+        series(3)
+        gain_r(1)
+        turn_x(1)
+        quant(0)
+        gain_r(3)
+        scale_h(2)
+        weave_t(0, 1)
+        weave_t(1, 0)
+        scale_x(1, 0)
+        k1t(1)
+        planes(1)
+        scale_x(1, 1)
+        weave_t(1, 1)
+        quant_t(0)
+        weave(1)
+        quant_t(1)
+        gain_r(2)
+        turn_x(2)
+        w2c, w2s = quant_w(q2r, "w2")
+        k_out(1)
+        z_sum(0, 0)
+        quant(1)
+        z_sum(0, 1)
+        z_out(0, 0)
+        k1t(2)
+        cast(3)
+        z_sum(1, 0)
+        z_out(0, 1)
+        planes(2)
+        weave(2)
+        turn_h(3)
+        scale_x(2, 0)
+        scale_x(2, 1)
+        mag(0, both)
+        z_sum(1, 1)
+        sign(0, both)
+        k_out(2)
+        cast(4)
+        add_b(0, both, nc.gpsimd)
+        z_out(1, 0)
+        turn_x(3)
+        scale_h(3)
+        z_out(1, 1)
+        quant(2)
+        turn_h(4)
+        finish(0, both)
+        load(3)
+        for n in range(3, NB - 1):
+            if n % 2 == 0 and n + 4 < NB:
                 load((n + 4) // 2)
-            if n < NB:
-                k1t(n)
-            if n - 1 < NB:
-                for j in range(2):
-                    z_sum(n - 1, j)
-            if n + 1 < NB:
-                scale_h(n + 1)
-                scale_x(n + 1, 0)
-                scale_x(n + 1, 1)
-            if n >= 2:
-                mag(n - 2)
-            if n < NB:
-                planes(n)
-            if n >= 2:
-                add_b(n - 2)
-                sign(n - 2)
-            if n - 1 < NB:
-                for j in range(2):
-                    z_out(n - 1, j)
-            if n < NB:
-                weave(n)
-                k_out(n)
-            if n + 1 < NB:
-                quant_h(n + 1)
-                quant_x(n + 1)
-            if n < NB:
-                quant_k(n)
-            if n >= 2:
-                finish(n - 2)
-            if n + 3 < NB:
-                cast(n + 3)
+            k1t(n)
+            z_sum(n - 1, 0)
+            z_sum(n - 1, 1)
+            scale_h(n + 1)
+            scale_x(n, 0)
+            scale_x(n, 1)
+            mag(n - 2, both)
+            planes(n)
+            add_b(n - 2, both, nc.gpsimd)
+            sign(n - 2, both)
+            z_out(n - 1, 0)
+            z_out(n - 1, 1)
+            weave(n)
+            k_out(n)
+            quant(n)
+            finish(n - 2, both)
             if n + 2 < NB:
-                turn(n + 2)
+                cast(n + 2)
+                turn_h(n + 2)
+            turn_x(n + 1)
+        z_sum(14, 0)
+        mag(13, both)
+        k1t(15)
+        z_sum(14, 1)
+        z_out(14, 0)
+        add_b(13, both, nc.gpsimd)
+        scale_x(15, 0)
+        planes(15)
+        mag(14, one)
+        scale_x(15, 1)
+        weave(15)
+        z_out(14, 1)
+        sign(13, both)
+        quant(15, 0, 2)
+        k_out(15)
+        sign(14, two)
+        quant(15, 3, 4)
+        mag(14, two)
+        z_sum(15, 0)
+        sign(14, one)
+        finish(13, both)
+        z_out(15, 0)
+        z_sum(15, 1)
+        mag(15, one)
+        add_b(14, one, nc.gpsimd)
+        z_out(15, 1)
+        sign(15, one)
+        finish(14, one)
+        add_b(14, two, nc.gpsimd)
+        mag(15, two)
+        finish(14, two)
+        add_b(15, one, nc.vector)
+        add_b(15, two, nc.vector)
+        finish(15, one)
+        sign(15, two)
+        finish(15, two)

@@ -48,11 +48,19 @@ def tile_skewexptaylorrecurrentstep_t_kernel(tc, h, x_bytes, x_scale, a, t, p, q
             x_in[c] = xin
             h_in[c] = hin
 
+        def wide(n):
+            if n not in xw:
+                w = sb.tile([P, 2, E], BF16, name="xw", bufs=4, align_bytes=64)
+                xw[n] = w
+            return xw[n]
+
+        def widen_a(n):
+            nc.vector.tensor_tensor(
+                out=wide(n)[:, 0, :], in0=x_in[n // 2][:].bitcast(FP8)[:, 2 * (n % 2), :], in1=xsb[:], op=ALU.mult
+            )
+
         def cast(n):
-            w = sb.tile([P, 2, E], BF16, name="xw", align_bytes=64)
-            j0 = 2 * (n % 2)
-            nc.scalar.copy(out=w[:], in_=x_in[n // 2][:].bitcast(FP8)[:, j0 : j0 + 2, :])
-            xw[n] = w
+            nc.scalar.copy(out=wide(n)[:, 1, :], in_=x_in[n // 2][:].bitcast(FP8)[:, 2 * (n % 2) + 1, :])
 
         def turn_h(n):
             j0 = 2 * (n % 2)
@@ -63,14 +71,13 @@ def tile_skewexptaylorrecurrentstep_t_kernel(tc, h, x_bytes, x_scale, a, t, p, q
                     nc.tensor.transpose(hb[:, u, j * P : (j + 1) * P], hw[:, j0 + j, u::2], ident_f[:])
             ht[n] = hb
 
-        def turn_x(n):
-            ww_ = xw[n][:].bitcast(F32)
+        def turn_x(n, j):
+            words = xw[n][:].bitcast(F32)
+            xb = ps.tile([P, 2, 2, P], F32, name="xt", bufs=2)
             for g in range(2):
-                xb = ps.tile([P, 2, BLK], F32, name="xt", bufs=2)
-                for j in range(2):
-                    for u in range(2):
-                        nc.tensor.transpose(xb[:, u, j * P : (j + 1) * P], ww_[:, j, 256 * g + u : 256 * (g + 1) : 2], ident_f[:])
-                xt[n, g] = xb
+                for u in range(2):
+                    nc.tensor.transpose(xb[:, g, u, :], words[:, j, 256 * g + u : 256 * (g + 1) : 2], ident_f[:])
+            xt[n, j] = xb
 
         def paired(bank):
             return bank[:].bitcast(BF16).rearrange("p u (r e) -> p r u e", e=2)
@@ -86,12 +93,21 @@ def tile_skewexptaylorrecurrentstep_t_kernel(tc, h, x_bytes, x_scale, a, t, p, q
 
         def scale_h(n):
             nc.vector.tensor_tensor(
-                out=stage(n - 1)[:, 2].rearrange("p r (u e) -> p r u e", u=2), in0=paired(ht[n]), in1=per_k(pg[:, 0, :]), op=ALU.mult
+                out=stage(n - 1)[:, 2].rearrange("p r (u e) -> p r u e", u=2), in0=per_k(pg[:, 0, :]), in1=paired(ht[n]), op=ALU.mult
             )
 
         def scale_x(n, g):
             nc.vector.tensor_tensor(
-                out=stage(n)[:, g].rearrange("p r (u e) -> p r u e", u=2), in0=paired(xt[n, g]), in1=per_k(xsc[:, g, :]), op=ALU.mult
+                out=stage(n)[:, g, P:, :].rearrange("p r (u e) -> p r u e", u=2),
+                in0=xsc[:, g, :].rearrange("p (u e) -> p u e", u=2).unsqueeze(1).to_broadcast([P, P, 2, 2]),
+                in1=xt[n, 1][:, g].bitcast(BF16).rearrange("p u (r e) -> p r u e", e=2),
+                op=ALU.mult,
+            )
+
+        def x_out(n):
+            nc.scalar.copy(
+                out=stage(n)[:, 0:2, 0:P, :].rearrange("p g r t -> p g (r t)").bitcast(F32).rearrange("p g (r u) -> p g r u", u=2),
+                in_=xt[n, 0][:].rearrange("p g u r -> p g r u"),
             )
 
         def quant(n, lo=0, hi=4):
@@ -134,12 +150,11 @@ def tile_skewexptaylorrecurrentstep_t_kernel(tc, h, x_bytes, x_scale, a, t, p, q
 
         def weave(n):
             bank = ps.tile([P, BLK, 4], BF16, name="kb")
-            for half in range(2):
-                cols = slice(half * P, (half + 1) * P)
+            for u in range(2):
                 nc.tensor.matmul(
-                    out=bank[:, cols, :].rearrange("p r t -> p (r t)"),
+                    out=bank[:, :, 2 * u : 2 * u + 2],
                     lhsT=ident_b[:],
-                    rhs=kp[n][:, :, cols].rearrange("p t r -> p r t"),
+                    rhs=kp[n][:, 2 * u : 2 * u + 2, :].rearrange("p t r -> p r t"),
                     start=True,
                     stop=True,
                 )
@@ -171,8 +186,8 @@ def tile_skewexptaylorrecurrentstep_t_kernel(tc, h, x_bytes, x_scale, a, t, p, q
                 zs[n] = o
             nc.vector.tensor_tensor(
                 out=zs[n][:, j, :].rearrange("p (m t) -> p m t", t=4),
-                in0=zp[n, j][:].rearrange("p (t m) -> p m t", t=4),
-                in1=h_in[n // 2][:, 2 * (n % 2) + j, :].rearrange("p (m t) -> p m t", t=4),
+                in0=h_in[n // 2][:, 2 * (n % 2) + j, :].rearrange("p (m t) -> p m t", t=4),
+                in1=zp[n, j][:].rearrange("p (t m) -> p m t", t=4),
                 op=ALU.add,
             )
 
@@ -207,6 +222,7 @@ def tile_skewexptaylorrecurrentstep_t_kernel(tc, h, x_bytes, x_scale, a, t, p, q
         a4 = keep.tile([P, 4, D], BF16, name="a4", align_bytes=64)
         pg = keep.tile([P, 3, 4], BF16, name="pg", align_bytes=64)
         qg = keep.tile([P, 3, 4], BF16, name="qg", align_bytes=64)
+        xsb = keep.tile([P, E], F32, name="xsb", align_bytes=64)
         xsc = keep.tile([P, 2, 4], F32, name="xsc", align_bytes=64)
         ident_b = keep.tile([P, P], BF16, name="ident_b", align_bytes=64)
         ident_f = keep.tile([P, P], F32, name="ident_f", align_bytes=64)
@@ -215,7 +231,7 @@ def tile_skewexptaylorrecurrentstep_t_kernel(tc, h, x_bytes, x_scale, a, t, p, q
         bias = keep.tile([P, D], BF16, name="bias", align_bytes=64)
         p1n = keep.tile([P, 4], F32, name="p1n", align_bytes=64)
         p2f = keep.tile([P, 4], F32, name="p2f", align_bytes=64)
-        q2h = keep.tile([P, 4], F32, name="q2h", align_bytes=64)
+        q2s = keep.tile([P, 4], F32, name="q2s", align_bytes=64)
         def kscale(vec, cols):
             return vec.unsqueeze(1).to_broadcast([P, cols, 4])
 
@@ -237,7 +253,7 @@ def tile_skewexptaylorrecurrentstep_t_kernel(tc, h, x_bytes, x_scale, a, t, p, q
 
         def gain_q0(cq):
             cols = slice(cq * P, (cq + 1) * P)
-            nc.vector.tensor_tensor(out=q0s[:, cols], in0=sbank[cq][:].rearrange("p t c -> p c t"), in1=kscale(qg[:, 0, :], P), op=ALU.mult)
+            nc.vector.tensor_tensor(out=q0s[:, cols], in0=kscale(qg[:, 0, :], P), in1=sbank[cq][:].rearrange("p t c -> p c t"), op=ALU.mult)
 
         def keep_s(cq):
             cols = slice(cq * P, (cq + 1) * P)
@@ -254,18 +270,8 @@ def tile_skewexptaylorrecurrentstep_t_kernel(tc, h, x_bytes, x_scale, a, t, p, q
             cols = slice(cq * P, (cq + 1) * P)
             nc.gpsimd.tensor_tensor(out=q1s[:, cols], in0=s_f[:, cols], in1=kscale(qg[:, 1, :], P), op=ALU.mult)
 
-        def weave_t(g, half):
-            bank = ps.tile([P, BLK, 4], BF16, name="tb", tag=("kb", "zb")[half], bufs=(1, 2)[half])
-            for i in range(2):
-                cq = 2 * half + i
-                nc.tensor.matmul(
-                    out=bank[:, i * P : (i + 1) * P, :].rearrange("p m j -> p (m j)"),
-                    lhsT=ident_b[:],
-                    rhs=t4[:, g, :, cq::4].rearrange("p j m -> p m j"),
-                    start=True,
-                    stop=True,
-                )
-            nc.scalar.copy(out=tg[:, g, half * BLK : (half + 1) * BLK, :], in_=bank[:])
+        def turn_t(g):
+            nc.scalar.copy(out=tg[:, g].rearrange("p (t m) j -> p t m j", t=4), in_=t4[:, g].rearrange("p j (m t) -> p t m j", t=4))
 
         def square(cq):
             cols = slice(cq * P, (cq + 1) * P)
@@ -286,9 +292,9 @@ def tile_skewexptaylorrecurrentstep_t_kernel(tc, h, x_bytes, x_scale, a, t, p, q
             cols = slice(cq * P, (cq + 1) * P)
             nc.vector.scalar_tensor_tensor(
                 out=r_f[:, cols, :],
-                in0=sq[cq][:].rearrange("p t c -> p c t"),
-                scalar=1.0 / 3.0,
-                in1=s_f[:, cols, :],
+                in0=s_f[:, cols, :],
+                scalar=3.0,
+                in1=sq[cq][:].rearrange("p t c -> p c t"),
                 op0=ALU.mult,
                 op1=ALU.add,
             )
@@ -296,11 +302,11 @@ def tile_skewexptaylorrecurrentstep_t_kernel(tc, h, x_bytes, x_scale, a, t, p, q
         sq = {}
         def gain_r(cq):
             cols = slice(cq * P, (cq + 1) * P)
-            nc.gpsimd.tensor_tensor(out=q2r[:, cols], in0=r_f[:, cols], in1=kscale(q2h[:], P), op=ALU.mult)
+            nc.gpsimd.tensor_tensor(out=q2r[:, cols], in0=r_f[:, cols], in1=kscale(q2s[:], P), op=ALU.mult)
 
         def gain_v(cq):
             cols = slice(cq * P, (cq + 1) * P)
-            nc.vector.tensor_tensor(out=p1s[:, cols], in0=sbank[cq][:].rearrange("p t c -> p c t"), in1=kscale(p1n[:], P), op=ALU.mult)
+            nc.vector.tensor_tensor(out=p1s[:, cols], in0=kscale(p1n[:], P), in1=sbank[cq][:].rearrange("p t c -> p c t"), op=ALU.mult)
 
         def quant_t(g):
             nc.vector.quantize_mx(out=tc_[:, g, :].bitcast(FP8X4), scales=ts_[:, g, :], in_=tg[:, g].rearrange("p c t -> p (c t)"))
@@ -309,171 +315,188 @@ def tile_skewexptaylorrecurrentstep_t_kernel(tc, h, x_bytes, x_scale, a, t, p, q
         two = slice(1, 2)
 
         make_identity(nc, ident_b[:])
-        nc.sync.dma_start(out=a4[:], in_=a.rearrange("(p j) n -> p j n", j=4))
         nc.vector.tensor_scalar(out=neg_b[:], in0=ident_b[:], scalar1=-1.0, scalar2=None, op0=ALU.mult)
+        nc.sync.dma_start(out=a4[:], in_=a.rearrange("(p j) n -> p j n", j=4))
+        make_identity(nc, ident_f[:])
         nc.scalar.dma_start(out=pg[:], in_=p.rearrange("g (p t) -> p g t", t=4))
+        skew(0)
+        nc.vector.tensor_copy(out=p2f[:], in_=pg[:, 2, :])
         nc.scalar.dma_start(out=qg[:], in_=q.rearrange("g (p t) -> p g t", t=4))
         nc.scalar.dma_start(out=xsc[:], in_=x_scale.rearrange("o (g p t) -> p (o g) t", p=P, t=4))
         nc.vector.tensor_scalar(out=p1n[:], in0=pg[:, 1, :], scalar1=-1.0, scalar2=None, op0=ALU.mult)
-        load(0)
-        skew(2)
-        nc.vector.tensor_copy(out=p2f[:], in_=pg[:, 2, :])
-        skew(0)
-        gain_q0(2)
         skew(1)
-        gain_q0(0)
-        keep_s(2)
-        gain_q0(1)
-        nc.sync.dma_start(out=t4[:], in_=t.rearrange("(g p j) n -> p g j n", p=P, j=4))
-        make_identity(nc, ident_f[:])
-        keep_s(0)
+        nc.sync.dma_start(out=xsb[:], in_=x_scale.rearrange("o k -> (o k)").partition_broadcast(P))
         skew(3)
+        skew(2)
+        nc.vector.tensor_scalar(out=q2s[:], in0=qg[:, 2, :], scalar1=1.0 / 6.0, scalar2=None, op0=ALU.mult)
+        load(0)
+        gain_q0(0)
+        gain_q0(1)
         turn_h(0)
-        gain_v(2)
+        keep_s(0)
+        gain_q0(3)
+        gain_v(0)
         keep_s(1)
+        nc.sync.dma_start(out=t4[:], in_=t.rearrange("(g p j) n -> p g j n", p=P, j=4))
+        gain_q1(0)
+        keep_s(3)
+        nc.sync.dma_start(out=bias[:], in_=b.partition_broadcast(P))
+        widen_a(0)
+        cast(0)
+        gain_q0(2)
+        keep_s(2)
+        gain_v(3)
+        gain_v(1)
+        gain_q1(1)
+        gain_v(2)
+        gain_q1(3)
+        gain_q1(2)
         scale_h(0)
         turn_h(1)
-        gain_q0(3)
-        keep_s(3)
-        quant(-1, 2, 3)
-        gain_q1(2)
         w0c, w0s = quant_w(q0s, "w0")
-        gain_v(3)
-        nc.sync.dma_start(out=bias[:], in_=b.partition_broadcast(P))
-        cast(0)
-        gain_q1(1)
-        k1t(0)
-        gain_q1(3)
-        gain_q1(0)
-        turn_x(0)
-        planes(0)
-        weave(0)
-        gain_v(1)
-        gain_v(0)
-        scale_h(1)
-        nc.vector.tensor_scalar(out=q2h[:], in0=qg[:, 2, :], scalar1=0.5, scalar2=None, op0=ALU.mult)
-        lc, ls = quant_w(p1s, "l1")
-        rc, rs = quant_w(q1s, "r1")
-        scale_x(0, 0)
-        square(1)
-        square(0)
-        series(0)
+        turn_x(0, 0)
         cast(1)
-        series(1)
+        quant(-1, 2, 3)
+        turn_t(0)
+        lc, ls = quant_w(p1s, "l1")
         load(1)
-        turn_h(2)
-        k_out(0)
-        square(2)
-        scale_x(0, 1)
-        cast(2)
-        weave_t(0, 0)
-        series(2)
+        rc, rs = quant_w(q1s, "r1")
+        x_out(0)
+        k1t(0)
+        square(0)
         load(2)
+        scale_h(1)
+        series(0)
+        widen_a(1)
+        square(1)
+        series(1)
+        square(2)
+        planes(0)
+        turn_x(0, 1)
+        scale_x(0, 0)
+        cast(3)
+        weave(0)
+        scale_x(0, 1)
+        series(2)
+        k_out(0)
+        turn_x(1, 1)
         square(3)
-        gain_r(0)
-        series(3)
-        gain_r(1)
-        turn_x(1)
+        turn_t(1)
+        turn_h(2)
+        cast(2)
         quant(0)
-        gain_r(3)
-        scale_h(2)
-        weave_t(0, 1)
-        weave_t(1, 0)
+        series(3)
+        turn_x(1, 0)
+        scale_x(1, 1)
         scale_x(1, 0)
         k1t(1)
+        gain_r(0)
+        gain_r(1)
         planes(1)
-        scale_x(1, 1)
-        weave_t(1, 1)
-        quant_t(0)
-        weave(1)
-        quant_t(1)
         gain_r(2)
-        turn_x(2)
-        w2c, w2s = quant_w(q2r, "w2")
+        x_out(1)
+        scale_h(2)
+        gain_r(3)
+        turn_x(2, 1)
+        weave(1)
+        turn_h(3)
         k_out(1)
-        z_sum(0, 0)
+        widen_a(2)
+        turn_x(2, 0)
+        w2c, w2s = quant_w(q2r, "w2")
+        quant_t(1)
+        quant_t(0)
         quant(1)
-        z_sum(0, 1)
+        z_sum(0, 0)
         z_out(0, 0)
         k1t(2)
-        cast(3)
-        z_sum(1, 0)
+        z_sum(0, 1)
+        x_out(2)
+        widen_a(3)
+        scale_h(3)
         z_out(0, 1)
         planes(2)
-        weave(2)
-        turn_h(3)
-        scale_x(2, 0)
-        scale_x(2, 1)
         mag(0, both)
-        z_sum(1, 1)
         sign(0, both)
-        k_out(2)
-        cast(4)
+        weave(2)
+        widen_a(4)
         add_b(0, both, nc.gpsimd)
+        z_sum(1, 0)
+        z_sum(1, 1)
         z_out(1, 0)
-        turn_x(3)
-        scale_h(3)
+        k_out(2)
+        scale_x(2, 1)
+        turn_h(4)
+        scale_x(2, 0)
         z_out(1, 1)
         quant(2)
-        turn_h(4)
         finish(0, both)
+        turn_x(3, 0)
+        cast(4)
         load(3)
+        turn_x(3, 1)
         for n in range(3, NB - 1):
+            scale_x(n, 1)
             if n % 2 == 0 and n + 4 < NB:
                 load((n + 4) // 2)
-            k1t(n)
+            scale_x(n, 0)
             z_sum(n - 1, 0)
+            k1t(n)
+            z_out(n - 1, 0)
+            mag(n - 2, both)
+            x_out(n)
+            planes(n)
             z_sum(n - 1, 1)
             scale_h(n + 1)
-            scale_x(n, 0)
-            scale_x(n, 1)
-            mag(n - 2, both)
-            planes(n)
-            add_b(n - 2, both, nc.gpsimd)
-            sign(n - 2, both)
-            z_out(n - 1, 0)
-            z_out(n - 1, 1)
             weave(n)
+            if n + 2 < NB:
+                turn_h(n + 2)
+            z_out(n - 1, 1)
+            sign(n - 2, both)
+            turn_x(n + 1, 1)
+            if n + 2 < NB:
+                widen_a(n + 2)
             k_out(n)
             quant(n)
+            add_b(n - 2, both, nc.gpsimd)
             finish(n - 2, both)
             if n + 2 < NB:
                 cast(n + 2)
-                turn_h(n + 2)
-            turn_x(n + 1)
-        z_sum(14, 0)
-        mag(13, both)
-        k1t(15)
-        z_sum(14, 1)
-        z_out(14, 0)
-        add_b(13, both, nc.gpsimd)
-        scale_x(15, 0)
-        planes(15)
-        mag(14, one)
-        scale_x(15, 1)
-        weave(15)
-        z_out(14, 1)
+            turn_x(n + 1, 0)
         sign(13, both)
+        z_sum(14, 1)
+        mag(13, both)
+        z_out(14, 1)
+        scale_x(15, 0)
+        k1t(15)
+        x_out(15)
+        planes(15)
+        add_b(13, both, nc.gpsimd)
+        z_sum(14, 0)
+        weave(15)
+        scale_x(15, 1)
+        z_out(14, 0)
         quant(15, 0, 2)
-        k_out(15)
-        sign(14, two)
-        quant(15, 3, 4)
-        mag(14, two)
-        z_sum(15, 0)
-        sign(14, one)
+        mag(14, one)
         finish(13, both)
+        k_out(15)
+        mag(14, two)
+        quant(15, 3, 4)
+        z_sum(15, 0)
         z_out(15, 0)
-        z_sum(15, 1)
-        mag(15, one)
-        add_b(14, one, nc.gpsimd)
-        z_out(15, 1)
-        sign(15, one)
-        finish(14, one)
         add_b(14, two, nc.gpsimd)
-        mag(15, two)
-        finish(14, two)
+        add_b(14, one, nc.gpsimd)
+        z_sum(15, 1)
+        sign(14, one)
+        z_out(15, 1)
+        mag(15, one)
         add_b(15, one, nc.vector)
+        mag(15, two)
         add_b(15, two, nc.vector)
-        finish(15, one)
+        sign(14, two)
+        finish(14, one)
+        sign(15, one)
         sign(15, two)
+        finish(14, two)
+        finish(15, one)
         finish(15, two)

@@ -65,7 +65,7 @@ def tile_skewexptaylorrecurrentstep_t_kernel(tc, h, x_bytes, x_scale, a, t, p, q
         def turn_h(n):
             j0 = 2 * (n % 2)
             hw = h_in[n // 2][:].bitcast(F32)
-            hb = ps.tile([P, 2, BLK], F32, name="ht")
+            hb = ps.tile([P, 2, BLK], F32, name="ht", bufs=2)
             for j in range(2):
                 for u in range(2):
                     nc.tensor.transpose(hb[:, u, j * P : (j + 1) * P], hw[:, j0 + j, u::2], ident_f[:])
@@ -148,20 +148,9 @@ def tile_skewexptaylorrecurrentstep_t_kernel(tc, h, x_bytes, x_scale, a, t, p, q
                 nc.scalar.activation(out=o[:, tt, :], in_=kt[n, tt // 2][:, tt % 2, :], func=ACT.Copy, scale=p2f[:, tt : tt + 1])
             kp[n] = o
 
-        def weave(n):
-            bank = ps.tile([P, BLK, 4], BF16, name="kb")
-            for u in range(2):
-                nc.tensor.matmul(
-                    out=bank[:, :, 2 * u : 2 * u + 2],
-                    lhsT=ident_b[:],
-                    rhs=kp[n][:, 2 * u : 2 * u + 2, :].rearrange("p t r -> p r t"),
-                    start=True,
-                    stop=True,
-                )
-            kq[n] = bank
-
-        def k_out(n):
-            nc.scalar.copy(out=stage(n)[:, 3], in_=kq[n][:])
+        def lace(n):
+            move = nc.vector.tensor_copy if n % 4 == 1 else nc.scalar.copy
+            move(out=stage(n)[:, 3], in_=kp[n][:].rearrange("p t r -> p r t"))
 
         def z_sum(n, j):
             bank = ps.tile([P, D], F32, name="zb", bufs=2)
@@ -270,8 +259,17 @@ def tile_skewexptaylorrecurrentstep_t_kernel(tc, h, x_bytes, x_scale, a, t, p, q
             cols = slice(cq * P, (cq + 1) * P)
             nc.gpsimd.tensor_tensor(out=q1s[:, cols], in0=s_f[:, cols], in1=kscale(qg[:, 1, :], P), op=ALU.mult)
 
-        def turn_t(g):
-            nc.scalar.copy(out=tg[:, g].rearrange("p (t m) j -> p t m j", t=4), in_=t4[:, g].rearrange("p j (m t) -> p t m j", t=4))
+        def weave_t(g, half):
+            bank = ps.tile([P, BLK, 4], BF16, name="tb", tag=("ht", "zb")[half], bufs=2)
+            for i in range(2):
+                nc.tensor.matmul(
+                    out=bank[:, i * P : (i + 1) * P, :].rearrange("p m j -> p (m j)"),
+                    lhsT=ident_b[:],
+                    rhs=t4[:, g, :, 2 * half + i :: 4].rearrange("p j m -> p m j"),
+                    start=True,
+                    stop=True,
+                )
+            nc.scalar.copy(out=tg[:, g, half * BLK : (half + 1) * BLK, :], in_=bank[:])
 
         def square(cq):
             cols = slice(cq * P, (cq + 1) * P)
@@ -314,189 +312,186 @@ def tile_skewexptaylorrecurrentstep_t_kernel(tc, h, x_bytes, x_scale, a, t, p, q
         one = slice(0, 1)
         two = slice(1, 2)
 
-        make_identity(nc, ident_b[:])
-        nc.vector.tensor_scalar(out=neg_b[:], in0=ident_b[:], scalar1=-1.0, scalar2=None, op0=ALU.mult)
         nc.sync.dma_start(out=a4[:], in_=a.rearrange("(p j) n -> p j n", j=4))
         make_identity(nc, ident_f[:])
+        make_identity(nc, ident_b[:])
         nc.scalar.dma_start(out=pg[:], in_=p.rearrange("g (p t) -> p g t", t=4))
+        nc.vector.tensor_scalar(out=neg_b[:], in0=ident_b[:], scalar1=-1.0, scalar2=None, op0=ALU.mult)
         skew(0)
-        nc.vector.tensor_copy(out=p2f[:], in_=pg[:, 2, :])
         nc.scalar.dma_start(out=qg[:], in_=q.rearrange("g (p t) -> p g t", t=4))
-        nc.scalar.dma_start(out=xsc[:], in_=x_scale.rearrange("o (g p t) -> p (o g) t", p=P, t=4))
+        nc.vector.tensor_scalar(out=q2s[:], in0=qg[:, 2, :], scalar1=1.0 / 6.0, scalar2=None, op0=ALU.mult)
+        nc.vector.tensor_copy(out=p2f[:], in_=pg[:, 2, :])
         nc.vector.tensor_scalar(out=p1n[:], in0=pg[:, 1, :], scalar1=-1.0, scalar2=None, op0=ALU.mult)
         skew(1)
-        nc.sync.dma_start(out=xsb[:], in_=x_scale.rearrange("o k -> (o k)").partition_broadcast(P))
         skew(3)
-        skew(2)
-        nc.vector.tensor_scalar(out=q2s[:], in0=qg[:, 2, :], scalar1=1.0 / 6.0, scalar2=None, op0=ALU.mult)
-        load(0)
+        nc.scalar.dma_start(out=xsc[:], in_=x_scale.rearrange("o (g p t) -> p (o g) t", p=P, t=4))
         gain_q0(0)
-        gain_q0(1)
+        nc.sync.dma_start(out=xsb[:], in_=x_scale.rearrange("o k -> (o k)").partition_broadcast(P))
+        skew(2)
+        load(0)
         turn_h(0)
+        gain_q0(1)
         keep_s(0)
+        widen_a(0)
         gain_q0(3)
-        gain_v(0)
+        cast(0)
         keep_s(1)
+        gain_q0(2)
+        gain_v(0)
+        keep_s(3)
+        gain_v(3)
+        turn_h(1)
         nc.sync.dma_start(out=t4[:], in_=t.rearrange("(g p j) n -> p g j n", p=P, j=4))
         gain_q1(0)
-        keep_s(3)
-        nc.sync.dma_start(out=bias[:], in_=b.partition_broadcast(P))
-        widen_a(0)
-        cast(0)
-        gain_q0(2)
-        keep_s(2)
-        gain_v(3)
-        gain_v(1)
-        gain_q1(1)
-        gain_v(2)
-        gain_q1(3)
-        gain_q1(2)
-        scale_h(0)
-        turn_h(1)
-        w0c, w0s = quant_w(q0s, "w0")
         turn_x(0, 0)
-        cast(1)
-        quant(-1, 2, 3)
-        turn_t(0)
-        lc, ls = quant_w(p1s, "l1")
-        load(1)
-        rc, rs = quant_w(q1s, "r1")
-        x_out(0)
-        k1t(0)
-        square(0)
-        load(2)
+        keep_s(2)
+        gain_v(1)
+        scale_h(0)
+        gain_v(2)
         scale_h(1)
-        series(0)
-        widen_a(1)
-        square(1)
-        series(1)
-        square(2)
-        planes(0)
-        turn_x(0, 1)
-        scale_x(0, 0)
+        cast(1)
+        nc.sync.dma_start(out=bias[:], in_=b.partition_broadcast(P))
+        load(1)
+        gain_q1(1)
+        w0c, w0s = quant_w(q0s, "w0")
+        gain_q1(3)
+        quant(-1, 2, 3)
         cast(3)
-        weave(0)
-        scale_x(0, 1)
-        series(2)
-        k_out(0)
+        weave_t(0, 1)
+        lc, ls = quant_w(p1s, "l1")
+        gain_q1(2)
+        rc, rs = quant_w(q1s, "r1")
+        weave_t(0, 0)
+        k1t(0)
+        widen_a(2)
+        square(0)
+        square(1)
+        x_out(0)
+        series(1)
+        planes(0)
+        load(2)
+        turn_x(0, 1)
         turn_x(1, 1)
+        lace(0)
+        widen_a(1)
+        series(0)
+        weave_t(1, 0)
+        square(2)
         square(3)
-        turn_t(1)
-        turn_h(2)
-        cast(2)
-        quant(0)
-        series(3)
-        turn_x(1, 0)
-        scale_x(1, 1)
-        scale_x(1, 0)
-        k1t(1)
-        gain_r(0)
         gain_r(1)
-        planes(1)
+        scale_x(0, 1)
+        turn_h(2)
+        scale_x(0, 0)
+        series(2)
+        gain_r(0)
+        quant(0)
         gain_r(2)
-        x_out(1)
+        series(3)
+        scale_x(1, 1)
+        turn_x(1, 0)
+        cast(2)
+        weave_t(1, 1)
+        scale_x(1, 0)
         scale_h(2)
         gain_r(3)
-        turn_x(2, 1)
-        weave(1)
-        turn_h(3)
-        k_out(1)
-        widen_a(2)
-        turn_x(2, 0)
-        w2c, w2s = quant_w(q2r, "w2")
-        quant_t(1)
         quant_t(0)
-        quant(1)
+        k1t(1)
+        x_out(1)
+        planes(1)
+        turn_h(3)
+        quant_t(1)
+        w2c, w2s = quant_w(q2r, "w2")
+        turn_x(2, 1)
+        turn_x(2, 0)
         z_sum(0, 0)
+        lace(1)
+        z_sum(0, 1)
+        quant(1)
+        cast(4)
         z_out(0, 0)
         k1t(2)
-        z_sum(0, 1)
-        x_out(2)
-        widen_a(3)
         scale_h(3)
-        z_out(0, 1)
-        planes(2)
-        mag(0, both)
-        sign(0, both)
-        weave(2)
-        widen_a(4)
-        add_b(0, both, nc.gpsimd)
         z_sum(1, 0)
-        z_sum(1, 1)
-        z_out(1, 0)
-        k_out(2)
+        z_out(0, 1)
+        x_out(2)
         scale_x(2, 1)
-        turn_h(4)
+        planes(2)
+        widen_a(3)
+        z_sum(1, 1)
+        mag(0, both)
         scale_x(2, 0)
-        z_out(1, 1)
-        quant(2)
-        finish(0, both)
         turn_x(3, 0)
-        cast(4)
+        add_b(0, both, nc.gpsimd)
+        z_out(1, 1)
+        lace(2)
+        sign(0, both)
+        z_out(1, 0)
+        quant(2)
+        turn_h(4)
+        finish(0, both)
         load(3)
         turn_x(3, 1)
+        widen_a(4)
         for n in range(3, NB - 1):
-            scale_x(n, 1)
+            scale_x(n, 0)
             if n % 2 == 0 and n + 4 < NB:
                 load((n + 4) // 2)
-            scale_x(n, 0)
-            z_sum(n - 1, 0)
             k1t(n)
+            scale_h(n + 1)
+            scale_x(n, 1)
+            x_out(n)
+            z_sum(n - 1, 0)
+            z_sum(n - 1, 1)
+            sign(n - 2, both)
             z_out(n - 1, 0)
             mag(n - 2, both)
-            x_out(n)
             planes(n)
-            z_sum(n - 1, 1)
-            scale_h(n + 1)
-            weave(n)
-            if n + 2 < NB:
-                turn_h(n + 2)
+            add_b(n - 2, both, nc.gpsimd)
             z_out(n - 1, 1)
-            sign(n - 2, both)
-            turn_x(n + 1, 1)
+            lace(n)
+            quant(n)
             if n + 2 < NB:
                 widen_a(n + 2)
-            k_out(n)
-            quant(n)
-            add_b(n - 2, both, nc.gpsimd)
-            finish(n - 2, both)
+            turn_x(n + 1, 1)
+            turn_x(n + 1, 0)
             if n + 2 < NB:
                 cast(n + 2)
-            turn_x(n + 1, 0)
-        sign(13, both)
+            if n + 2 < NB:
+                turn_h(n + 2)
+            finish(n - 2, both)
         z_sum(14, 1)
         mag(13, both)
-        z_out(14, 1)
-        scale_x(15, 0)
         k1t(15)
         x_out(15)
-        planes(15)
-        add_b(13, both, nc.gpsimd)
+        scale_x(15, 0)
         z_sum(14, 0)
-        weave(15)
+        sign(13, both)
         scale_x(15, 1)
-        z_out(14, 0)
+        z_out(14, 1)
+        planes(15)
+        lace(15)
         quant(15, 0, 2)
+        add_b(13, both, nc.gpsimd)
+        z_out(14, 0)
         mag(14, one)
-        finish(13, both)
-        k_out(15)
-        mag(14, two)
-        quant(15, 3, 4)
-        z_sum(15, 0)
-        z_out(15, 0)
-        add_b(14, two, nc.gpsimd)
-        add_b(14, one, nc.gpsimd)
-        z_sum(15, 1)
-        sign(14, one)
-        z_out(15, 1)
-        mag(15, one)
-        add_b(15, one, nc.vector)
-        mag(15, two)
-        add_b(15, two, nc.vector)
         sign(14, two)
+        quant(15, 3, 4)
+        finish(13, both)
+        z_sum(15, 0)
+        z_sum(15, 1)
+        mag(14, two)
+        sign(14, one)
+        add_b(14, one, nc.gpsimd)
+        z_out(15, 0)
+        z_out(15, 1)
+        add_b(14, two, nc.gpsimd)
+        mag(15, one)
+        mag(15, two)
         finish(14, one)
-        sign(15, one)
         sign(15, two)
+        add_b(15, one, nc.vector)
         finish(14, two)
+        add_b(15, two, nc.vector)
+        sign(15, one)
         finish(15, one)
         finish(15, two)

from contextlib import ExitStack

import concourse.mybir as mybir
from concourse.masks import make_identity

F32 = mybir.dt.float32
BF16 = mybir.dt.bfloat16
U32 = mybir.dt.uint32
U8 = mybir.dt.uint8
FP8 = mybir.dt.float8_e4m3fn
FP8X4 = mybir.dt.float8_e4m3fn_x4
ALU = mybir.AluOpType
ACT = mybir.ActivationFunctionType

N, D, E, G = 4096, 512, 1024, 3
FLOPS = 2 * N * D * (2 * D + E) + 2 * D * D * D

P = 128
CHUNK = 512
BLK = 256
NB = N // BLK


def tile_skewexptaylorrecurrentstep_t_kernel(tc, h, x_bytes, x_scale, a, t, p, q, b, out):
    nc = tc.nc
    h_v = h.rearrange("(i p j) k -> i p j k", p=P, j=4)
    x_v = x_bytes.rearrange("(i p j) k -> i p j k", p=P, j=4)
    o_v = out.rearrange("(i p j) k -> i p j k", p=P, j=4)

    with ExitStack() as ctx:
        keep = ctx.enter_context(tc.tile_pool(name="keep", bufs=1))
        io = ctx.enter_context(tc.tile_pool(name="io", bufs=4))
        sb = ctx.enter_context(tc.tile_pool(name="sb", bufs=3))
        ps = ctx.enter_context(tc.psum_pool(name="ps", bufs=1))
        ctx.enter_context(tc.manual_schedule())

        x_in, h_in = {}, {}
        xw, xt, ht, kq = {}, {}, {}, {}
        qin, codes = {}, {}
        kt, kp = {}, {}
        zp, zs, az, sg, ww, rs_ = {}, {}, {}, {}, {}, {}

        def load(c):
            xin = io.tile([P, 4, E], U8, name="xin", align_bytes=64)
            nc.sync.dma_start(out=xin[:], in_=x_v[c])
            hin = io.tile([P, 4, D], BF16, name="hin", align_bytes=64)
            nc.sync.dma_start(out=hin[:], in_=h_v[c])
            x_in[c] = xin
            h_in[c] = hin

        def wide(n):
            if n not in xw:
                w = sb.tile([P, 2, E], BF16, name="xw", bufs=4, align_bytes=64)
                xw[n] = w
            return xw[n]

        def widen_a(n):
            nc.vector.tensor_tensor(
                out=wide(n)[:, 0, :], in0=x_in[n // 2][:].bitcast(FP8)[:, 2 * (n % 2), :], in1=xsb[:], op=ALU.mult
            )

        def cast(n):
            nc.scalar.copy(out=wide(n)[:, 1, :], in_=x_in[n // 2][:].bitcast(FP8)[:, 2 * (n % 2) + 1, :])

        def turn_h(n):
            j0 = 2 * (n % 2)
            hw = h_in[n // 2][:].bitcast(F32)
            hb = ps.tile([P, 2, BLK], F32, name="ht", bufs=2)
            for j in range(2):
                for u in range(2):
                    nc.tensor.transpose(hb[:, u, j * P : (j + 1) * P], hw[:, j0 + j, u::2], ident_f[:])
            ht[n] = hb

        def turn_x(n, j):
            words = xw[n][:].bitcast(F32)
            xb = ps.tile([P, 2, 2, P], F32, name="xt", bufs=2)
            for g in range(2):
                for u in range(2):
                    nc.tensor.transpose(xb[:, g, u, :], words[:, j, 256 * g + u : 256 * (g + 1) : 2], ident_f[:])
            xt[n, j] = xb

        def paired(bank):
            return bank[:].bitcast(BF16).rearrange("p u (r e) -> p r u e", e=2)

        def per_k(vec):
            return vec.rearrange("p (u e) -> p u e", u=2).unsqueeze(1).to_broadcast([P, BLK, 2, 2])

        def stage(n):
            if n not in qin:
                tile = sb.tile([P, 4, BLK, 4], BF16, name="qin", align_bytes=64)
                qin[n] = tile
            return qin[n]

        def scale_h(n):
            nc.vector.tensor_tensor(
                out=stage(n - 1)[:, 2].rearrange("p r (u e) -> p r u e", u=2), in0=per_k(pg[:, 0, :]), in1=paired(ht[n]), op=ALU.mult
            )

        def scale_x(n, g):
            nc.vector.tensor_tensor(
                out=stage(n)[:, g, P:, :].rearrange("p r (u e) -> p r u e", u=2),
                in0=xsc[:, g, :].rearrange("p (u e) -> p u e", u=2).unsqueeze(1).to_broadcast([P, P, 2, 2]),
                in1=xt[n, 1][:, g].bitcast(BF16).rearrange("p u (r e) -> p r u e", e=2),
                op=ALU.mult,
            )

        def x_out(n):
            nc.scalar.copy(
                out=stage(n)[:, 0:2, 0:P, :].rearrange("p g r t -> p g (r t)").bitcast(F32).rearrange("p g (r u) -> p g r u", u=2),
                in_=xt[n, 0][:].rearrange("p g u r -> p g r u"),
            )

        def quant(n, lo=0, hi=4):
            if n not in codes:
                c = sb.tile([P, 4, BLK], U32, name="codes", bufs=5, align_bytes=64)
                sc = sb.tile([P, 4, BLK], U8, name="scales", bufs=5, align_bytes=64)
                codes[n] = (c, sc)
            c, sc = codes[n]
            nc.vector.quantize_mx(
                out=c[:, lo:hi].rearrange("p o r -> p (o r)").bitcast(FP8X4),
                scales=sc[:, lo:hi].rearrange("p o r -> p (o r)"),
                in_=qin[n][:, lo:hi].rearrange("p o r t -> p (o r t)"),
            )

        def part(n, o, cols):
            c, sc = codes[n - 1 if o == 2 else n]
            return c[:, o, cols].bitcast(FP8X4), sc[:, o, cols]

        def k1t(n):
            for half in range(2):
                bank = ps.tile([P, 2, BLK], F32, name="kt", bufs=2)
                for i in range(2):
                    tt = 2 * half + i
                    nc.tensor.matmul_mx(
                        out=bank[:, i, :],
                        lhsT=w0c[:, tt * P : (tt + 1) * P].bitcast(FP8X4),
                        lhsT_scale=w0s[:, tt * P : (tt + 1) * P],
                        rhs=part(n, 2, slice(0, BLK))[0],
                        rhs_scale=part(n, 2, slice(0, BLK))[1],
                        start=True,
                        stop=True,
                    )
                kt[n, half] = bank

        def planes(n):
            o = sb.tile([P, 4, BLK], BF16, name="kp", bufs=2, align_bytes=64)
            for tt in range(4):
                nc.scalar.activation(out=o[:, tt, :], in_=kt[n, tt // 2][:, tt % 2, :], func=ACT.Copy, scale=p2f[:, tt : tt + 1])
            kp[n] = o

        def lace(n):
            move = nc.vector.tensor_copy if n % 4 == 1 else nc.scalar.copy
            move(out=stage(n)[:, 3], in_=kp[n][:].rearrange("p t r -> p r t"))

        def z_sum(n, j):
            bank = ps.tile([P, D], F32, name="zb", bufs=2)
            cols = slice(j * P, (j + 1) * P)
            left = [part(n, 2, cols), part(n, 0, cols), part(n, 1, cols), part(n, 3, cols)]
            right = [(w0c[:], w0s[:]), (tc_[:, 0, :], ts_[:, 0, :]), (tc_[:, 1, :], ts_[:, 1, :]), (w2c[:], w2s[:])]
            for i in range(4):
                nc.tensor.matmul_mx(
                    out=bank[:],
                    lhsT=left[i][0],
                    lhsT_scale=left[i][1],
                    rhs=right[i][0].bitcast(FP8X4),
                    rhs_scale=right[i][1],
                    start=(i == 0),
                    stop=(i == 3),
                )
            zp[n, j] = bank

        def z_out(n, j):
            if n not in zs:
                o = sb.tile([P, 2, D], F32, name="zs", align_bytes=64)
                zs[n] = o
            nc.vector.tensor_tensor(
                out=zs[n][:, j, :].rearrange("p (m t) -> p m t", t=4),
                in0=h_in[n // 2][:, 2 * (n % 2) + j, :].rearrange("p (m t) -> p m t", t=4),
                in1=zp[n, j][:].rearrange("p (t m) -> p m t", t=4),
                op=ALU.add,
            )

        def mag(n, js):
            if n not in az:
                o = sb.tile([P, 2, D], F32, name="az", bufs=2, align_bytes=64)
                az[n] = o
            nc.scalar.activation(out=az[n][:, js], in_=zs[n][:, js], func=ACT.Abs)

        def sign(n, js):
            if n not in sg:
                o = sb.tile([P, 2, D], BF16, name="sg", bufs=2, align_bytes=64)
                sg[n] = o
            nc.scalar.activation(out=sg[n][:, js], in_=zs[n][:, js], func=ACT.Sign)

        def add_b(n, js, eng):
            if n not in ww:
                o = sb.tile([P, 2, D], F32, name="wb", bufs=2, align_bytes=64)
                ww[n] = o
            cnt = js.stop - js.start
            eng.tensor_tensor(out=ww[n][:, js], in0=az[n][:, js], in1=bias[:].unsqueeze(1).to_broadcast([P, cnt, D]), op=ALU.add)

        def finish(n, js):
            if n not in rs_:
                o = sb.tile([P, 2, D], F32, name="res", align_bytes=64)
                rs_[n] = o
            nc.vector.scalar_tensor_tensor(out=rs_[n][:, js], in0=ww[n][:, js], scalar=0.0, in1=sg[n][:, js], op0=ALU.max, op1=ALU.mult)
            j0 = 2 * (n % 2)
            nc.sync.dma_start(out=o_v[n // 2][:, j0 + js.start : j0 + js.stop, :], in_=rs_[n][:, js])

        both = slice(0, 2)
        a4 = keep.tile([P, 4, D], BF16, name="a4", align_bytes=64)
        pg = keep.tile([P, 3, 4], BF16, name="pg", align_bytes=64)
        qg = keep.tile([P, 3, 4], BF16, name="qg", align_bytes=64)
        xsb = keep.tile([P, E], F32, name="xsb", align_bytes=64)
        xsc = keep.tile([P, 2, 4], F32, name="xsc", align_bytes=64)
        ident_b = keep.tile([P, P], BF16, name="ident_b", align_bytes=64)
        ident_f = keep.tile([P, P], F32, name="ident_f", align_bytes=64)
        neg_b = keep.tile([P, P], BF16, name="neg_b", align_bytes=64)
        t4 = keep.tile([P, 2, 4, D], BF16, name="t4", align_bytes=64)
        bias = keep.tile([P, D], BF16, name="bias", align_bytes=64)
        p1n = keep.tile([P, 4], F32, name="p1n", align_bytes=64)
        p2f = keep.tile([P, 4], F32, name="p2f", align_bytes=64)
        q2s = keep.tile([P, 4], F32, name="q2s", align_bytes=64)
        def kscale(vec, cols):
            return vec.unsqueeze(1).to_broadcast([P, cols, 4])

        def quant_w(src, name):
            c = keep.tile([P, D], U32, name=name + "c", align_bytes=64)
            s = keep.tile([P, D], U8, name=name + "s", align_bytes=64)
            nc.vector.quantize_mx(out=c[:].bitcast(FP8X4), scales=s[:], in_=src[:].rearrange("p c t -> p (c t)"))
            return c, s

        s_f = keep.tile([P, D, 4], F32, name="s_f", align_bytes=64)
        q0s = keep.tile([P, D, 4], BF16, name="q0s", align_bytes=64)
        sbank = {}
        def skew(cq):
            bank = ps.tile([P, 4, P], F32, name="sbank", tag=("zb", "xt")[cq // 2], bufs=2)
            for tt in range(4):
                nc.tensor.matmul(out=bank[:, tt, :], lhsT=ident_b[:], rhs=a4[:, tt, cq::4], start=True, stop=False)
                nc.tensor.matmul(out=bank[:, tt, :], lhsT=a4[:, cq, tt::4], rhs=neg_b[:], start=False, stop=True)
            sbank[cq] = bank

        def gain_q0(cq):
            cols = slice(cq * P, (cq + 1) * P)
            nc.vector.tensor_tensor(out=q0s[:, cols], in0=kscale(qg[:, 0, :], P), in1=sbank[cq][:].rearrange("p t c -> p c t"), op=ALU.mult)

        def keep_s(cq):
            cols = slice(cq * P, (cq + 1) * P)
            nc.scalar.copy(out=s_f[:, cols], in_=sbank[cq][:].rearrange("p t c -> p c t"))

        p1s = keep.tile([P, D, 4], BF16, name="p1s", align_bytes=64)
        q1s = keep.tile([P, D, 4], BF16, name="q1s", align_bytes=64)
        tg = keep.tile([P, 2, D, 4], BF16, name="tg", align_bytes=64)
        tc_ = keep.tile([P, 2, D], U32, name="tc", align_bytes=64)
        ts_ = keep.tile([P, 2, D], U8, name="ts", align_bytes=64)
        r_f = keep.tile([P, D, 4], F32, name="r_f", align_bytes=64)
        q2r = keep.tile([P, D, 4], BF16, name="q2r", align_bytes=64)
        def gain_q1(cq):
            cols = slice(cq * P, (cq + 1) * P)
            nc.gpsimd.tensor_tensor(out=q1s[:, cols], in0=s_f[:, cols], in1=kscale(qg[:, 1, :], P), op=ALU.mult)

        def weave_t(g, half):
            bank = ps.tile([P, BLK, 4], BF16, name="tb", tag=("ht", "zb")[half], bufs=2)
            for i in range(2):
                nc.tensor.matmul(
                    out=bank[:, i * P : (i + 1) * P, :].rearrange("p m j -> p (m j)"),
                    lhsT=ident_b[:],
                    rhs=t4[:, g, :, 2 * half + i :: 4].rearrange("p j m -> p m j"),
                    start=True,
                    stop=True,
                )
            nc.scalar.copy(out=tg[:, g, half * BLK : (half + 1) * BLK, :], in_=bank[:])

        def square(cq):
            cols = slice(cq * P, (cq + 1) * P)
            bank = ps.tile([P, 4, P], F32, name="s2", tag="zb", bufs=2)
            for tt in range(4):
                nc.tensor.matmul_mx(
                    out=bank[:, tt, :],
                    lhsT=lc[:, tt * P : (tt + 1) * P].bitcast(FP8X4),
                    lhsT_scale=ls[:, tt * P : (tt + 1) * P],
                    rhs=rc[:, cols].bitcast(FP8X4),
                    rhs_scale=rs[:, cols],
                    start=True,
                    stop=True,
                )
            sq[cq] = bank

        def series(cq):
            cols = slice(cq * P, (cq + 1) * P)
            nc.vector.scalar_tensor_tensor(
                out=r_f[:, cols, :],
                in0=s_f[:, cols, :],
                scalar=3.0,
                in1=sq[cq][:].rearrange("p t c -> p c t"),
                op0=ALU.mult,
                op1=ALU.add,
            )

        sq = {}
        def gain_r(cq):
            cols = slice(cq * P, (cq + 1) * P)
            nc.gpsimd.tensor_tensor(out=q2r[:, cols], in0=r_f[:, cols], in1=kscale(q2s[:], P), op=ALU.mult)

        def gain_v(cq):
            cols = slice(cq * P, (cq + 1) * P)
            nc.vector.tensor_tensor(out=p1s[:, cols], in0=kscale(p1n[:], P), in1=sbank[cq][:].rearrange("p t c -> p c t"), op=ALU.mult)

        def quant_t(g):
            nc.vector.quantize_mx(out=tc_[:, g, :].bitcast(FP8X4), scales=ts_[:, g, :], in_=tg[:, g].rearrange("p c t -> p (c t)"))

        one = slice(0, 1)
        two = slice(1, 2)

        nc.sync.dma_start(out=a4[:], in_=a.rearrange("(p j) n -> p j n", j=4))
        make_identity(nc, ident_f[:])
        make_identity(nc, ident_b[:])
        nc.scalar.dma_start(out=pg[:], in_=p.rearrange("g (p t) -> p g t", t=4))
        nc.vector.tensor_scalar(out=neg_b[:], in0=ident_b[:], scalar1=-1.0, scalar2=None, op0=ALU.mult)
        skew(0)
        nc.scalar.dma_start(out=qg[:], in_=q.rearrange("g (p t) -> p g t", t=4))
        nc.vector.tensor_scalar(out=q2s[:], in0=qg[:, 2, :], scalar1=1.0 / 6.0, scalar2=None, op0=ALU.mult)
        nc.vector.tensor_copy(out=p2f[:], in_=pg[:, 2, :])
        nc.vector.tensor_scalar(out=p1n[:], in0=pg[:, 1, :], scalar1=-1.0, scalar2=None, op0=ALU.mult)
        skew(1)
        skew(3)
        nc.scalar.dma_start(out=xsc[:], in_=x_scale.rearrange("o (g p t) -> p (o g) t", p=P, t=4))
        gain_q0(0)
        nc.sync.dma_start(out=xsb[:], in_=x_scale.rearrange("o k -> (o k)").partition_broadcast(P))
        skew(2)
        load(0)
        turn_h(0)
        gain_q0(1)
        keep_s(0)
        widen_a(0)
        gain_q0(3)
        cast(0)
        keep_s(1)
        gain_q0(2)
        gain_v(0)
        keep_s(3)
        gain_v(3)
        turn_h(1)
        nc.sync.dma_start(out=t4[:], in_=t.rearrange("(g p j) n -> p g j n", p=P, j=4))
        gain_q1(0)
        turn_x(0, 0)
        keep_s(2)
        gain_v(1)
        scale_h(0)
        gain_v(2)
        scale_h(1)
        cast(1)
        nc.sync.dma_start(out=bias[:], in_=b.partition_broadcast(P))
        load(1)
        gain_q1(1)
        w0c, w0s = quant_w(q0s, "w0")
        gain_q1(3)
        quant(-1, 2, 3)
        cast(3)
        weave_t(0, 1)
        lc, ls = quant_w(p1s, "l1")
        gain_q1(2)
        rc, rs = quant_w(q1s, "r1")
        weave_t(0, 0)
        k1t(0)
        widen_a(2)
        square(0)
        square(1)
        x_out(0)
        series(1)
        planes(0)
        load(2)
        turn_x(0, 1)
        turn_x(1, 1)
        lace(0)
        widen_a(1)
        series(0)
        weave_t(1, 0)
        square(2)
        square(3)
        gain_r(1)
        scale_x(0, 1)
        turn_h(2)
        scale_x(0, 0)
        series(2)
        gain_r(0)
        quant(0)
        gain_r(2)
        series(3)
        scale_x(1, 1)
        turn_x(1, 0)
        cast(2)
        weave_t(1, 1)
        scale_x(1, 0)
        scale_h(2)
        gain_r(3)
        quant_t(0)
        k1t(1)
        x_out(1)
        planes(1)
        turn_h(3)
        quant_t(1)
        w2c, w2s = quant_w(q2r, "w2")
        turn_x(2, 1)
        turn_x(2, 0)
        z_sum(0, 0)
        lace(1)
        z_sum(0, 1)
        quant(1)
        cast(4)
        z_out(0, 0)
        k1t(2)
        scale_h(3)
        z_sum(1, 0)
        z_out(0, 1)
        x_out(2)
        scale_x(2, 1)
        planes(2)
        widen_a(3)
        z_sum(1, 1)
        mag(0, both)
        scale_x(2, 0)
        turn_x(3, 0)
        add_b(0, both, nc.gpsimd)
        z_out(1, 1)
        lace(2)
        sign(0, both)
        z_out(1, 0)
        quant(2)
        turn_h(4)
        finish(0, both)
        load(3)
        turn_x(3, 1)
        widen_a(4)
        for n in range(3, NB - 1):
            scale_x(n, 0)
            if n % 2 == 0 and n + 4 < NB:
                load((n + 4) // 2)
            k1t(n)
            scale_h(n + 1)
            scale_x(n, 1)
            x_out(n)
            z_sum(n - 1, 0)
            z_sum(n - 1, 1)
            sign(n - 2, both)
            z_out(n - 1, 0)
            mag(n - 2, both)
            planes(n)
            add_b(n - 2, both, nc.gpsimd)
            z_out(n - 1, 1)
            lace(n)
            quant(n)
            if n + 2 < NB:
                widen_a(n + 2)
            turn_x(n + 1, 1)
            turn_x(n + 1, 0)
            if n + 2 < NB:
                cast(n + 2)
            if n + 2 < NB:
                turn_h(n + 2)
            finish(n - 2, both)
        z_sum(14, 1)
        mag(13, both)
        k1t(15)
        x_out(15)
        scale_x(15, 0)
        z_sum(14, 0)
        sign(13, both)
        scale_x(15, 1)
        z_out(14, 1)
        planes(15)
        lace(15)
        quant(15, 0, 2)
        add_b(13, both, nc.gpsimd)
        z_out(14, 0)
        mag(14, one)
        sign(14, two)
        quant(15, 3, 4)
        finish(13, both)
        z_sum(15, 0)
        z_sum(15, 1)
        mag(14, two)
        sign(14, one)
        add_b(14, one, nc.gpsimd)
        z_out(15, 0)
        z_out(15, 1)
        add_b(14, two, nc.gpsimd)
        mag(15, one)
        mag(15, two)
        finish(14, one)
        sign(15, two)
        add_b(15, one, nc.vector)
        finish(14, two)
        add_b(15, two, nc.vector)
        sign(15, one)
        finish(15, one)
        finish(15, two)
